import numpy as np
import ml_dtypes


def mxq(x, axis, fmt="e4m3"):
    dtype, down = {"e4m3": (ml_dtypes.float8_e4m3fn, 7), "e5m2": (ml_dtypes.float8_e5m2, 14)}[fmt]
    v = np.moveaxis(np.asarray(x, np.float32).astype(ml_dtypes.bfloat16).astype(np.float64), axis, -1)
    blocks = v.reshape(v.shape[:-1] + (-1, 32))
    amax = np.abs(blocks).max(-1, keepdims=True)
    byte = np.maximum(np.where(amax > 0, np.frexp(amax)[1] - 1 + 127, 0) - down, 1)
    scale = np.exp2(byte - 127.0)
    codes = (blocks / scale).astype(np.float32).astype(dtype).astype(np.float64)
    return np.moveaxis((codes * scale).reshape(v.shape), -1, axis)


WIDE = False


def mx_kscale(k):
    if not WIDE:
        return np.ones(k)
    levels = np.array([10, -10, 5, -5, 0])
    if k % 512:
        return np.exp2(np.random.permutation(np.resize(levels, k // 32))).repeat(32)
    a = np.empty((k // 512, 16))
    for p in range(k // 512):
        a[p, :8] = np.random.permutation(np.resize(levels, 8))
        for g in range(8):
            far = levels[np.abs(levels - a[p, g]) >= 10]
            a[p, g + 8] = far[np.random.randint(len(far))]
    return np.exp2(a.ravel()).repeat(32)


def f64(x):
    return np.asarray(x).astype(np.float64)


def striped(idx):
    return np.tile(idx.reshape(-1, 16).T, (8, 1)).astype(np.uint16)


def unstriped(offs):
    return offs[:16].T.reshape(-1).astype(np.int64)


E2M1 = np.array([0.0, 0.5, 1.0, 1.5, 2.0, 3.0, 4.0, 6.0, -0.0, -0.5, -1.0, -1.5, -2.0, -3.0, -4.0, -6.0])


def pack_weight(w, fmt):
    k, n = w.shape
    w = f64(np.asarray(w, np.float32).astype(ml_dtypes.bfloat16)).reshape(k // 32, 32, n)
    amax = np.abs(w).max(1)
    if fmt == "e4m3":
        byte = np.frexp(amax)[1] - 1 + 127 - 7
    else:
        mant, ex = np.frexp(amax / 6.0)
        byte = np.where(mant > 0.5, ex, ex - 1) + 127
    byte = np.clip(np.where(amax > 0, byte, 1), 1, 254)
    scaled = (w * np.exp2(127.0 - byte)[:, None, :]).reshape(k, n).astype(np.float32)
    by_word = np.ascontiguousarray(scaled.reshape(k // 512, 128, 4, n).transpose(0, 1, 3, 2))
    if fmt == "e4m3":
        words = by_word.astype(ml_dtypes.float8_e4m3fn).view(np.uint8)
    else:
        c = by_word.astype(ml_dtypes.float4_e2m1fn).view(np.uint8) & 0xF
        words = (c[..., 0::2] | (c[..., 1::2] << 4)).reshape(k // 512, 128, 2 * n)
    return np.ascontiguousarray(words), np.ascontiguousarray(byte.astype(np.uint8).reshape(k // 512, 16, n))


def unpack_weight(words, scales, fmt):
    g, _, n = scales.shape
    words = np.ascontiguousarray(words).reshape(g, 128, n, -1)
    if fmt == "e4m3":
        vals = words.view(ml_dtypes.float8_e4m3fn).astype(np.float64)
    else:
        nib = np.empty((g, 128, n, 4), np.uint8)
        nib[..., 0::2] = words & 0xF
        nib[..., 1::2] = words >> 4
        vals = E2M1[nib]
    vals = vals * np.repeat(np.exp2(scales.astype(np.float64) - 127.0), 8, axis=1)[..., None]
    return vals.transpose(0, 1, 3, 2).reshape(g * 512, n)


def gelu(v):
    return 0.5 * v * (1.0 + np.tanh(np.sqrt(2.0 / np.pi) * (v + 0.044715 * v**3)))


def bf(x):
    return np.asarray(x, np.float32).astype(ml_dtypes.bfloat16)


def planes(Y):
    n, m = Y.shape
    b = f64(bf(Y)).reshape(n // 32, 32, m)
    amax = np.abs(b).max(1)
    byte = np.clip(np.where(amax > 0, np.frexp(amax)[1] - 1 + 127 - 7, 1), 1, 254)
    codes = (b * np.exp2(127.0 - byte)[:, None, :]).reshape(n, m).astype(np.float32).astype(ml_dtypes.float8_e4m3fn).view(np.uint8)
    words = codes.reshape(n // 512, 128, 4, m).transpose(0, 1, 3, 2)
    return np.ascontiguousarray(words), np.ascontiguousarray(byte.astype(np.uint8).reshape(n // 512, 16, m))


T, S, K, H, N = 2048, 1024, 1024, 512, 768

def setup_inputs():
    n = np.random.standard_normal
    s = mx_kscale(K)[:, None]
    u = mx_kscale(H)[:, None]
    tab_words, tab_scales = pack_weight(n((K, T)) * s, "e4m3")
    offs = striped(np.random.permutation(T)[:S])
    wa = (n((K, H)) / np.sqrt(K) / s * u.T).astype(np.float32)
    wb_words, wb_scales = pack_weight(n((K, H)) / np.sqrt(K) / s * u.T, "e2m1")
    wy = (0.7 * n((H, N)) / np.sqrt(H) / u).astype(np.float32)
    wd_words, wd_scales = pack_weight(0.6 * n((K, N)) / np.sqrt(K) / s, "e4m3")
    by = (0.3 * n(N)).astype(np.float32)
    return {"tab_words": tab_words, "tab_scales": tab_scales, "offs": offs,
            "wa": wa, "wb_words": wb_words, "wb_scales": wb_scales,
            "wy": wy, "wd_words": wd_words, "wd_scales": wd_scales, "by": by}

def reference(tab_words, tab_scales, offs, wa, wb_words, wb_scales, wy, wd_words, wd_scales, by):
    v = unpack_weight(tab_words, tab_scales, "e4m3")[:, unstriped(offs)]
    wb = unpack_weight(wb_words, wb_scales, "e2m1")
    wd = unpack_weight(wd_words, wd_scales, "e4m3")
    a = mxq(f64(wa), 0, "e4m3").T @ v
    b = wb.T @ v
    h = np.maximum(a, b)
    words, scales = planes(h)
    hq = mxq(h, 0, "e4m3")
    d = mxq(f64(wy), 0, "e4m3").T @ hq + wd.T @ v
    y = np.tanh(d + f64(by)[:, None])
    return y, h, words, scales

@@ -1,0 +1,256 @@
+from contextlib import ExitStack
+
+import concourse.mybir as mybir
+
+T, S, K, H, N = 2048, 1024, 1024, 512, 768
+FLOPS = 2 * S * (2 * K * H + H * N + K * N)
+
+F32 = mybir.dt.float32
+BF16 = mybir.dt.bfloat16
+I32 = mybir.dt.int32
+U32 = mybir.dt.uint32
+U16 = mybir.dt.uint16
+U8 = mybir.dt.uint8
+FP8X4 = mybir.dt.float8_e4m3fn_x4
+FP4X4 = mybir.dt.float4_e2m1fn_x4
+COPY = mybir.ActivationFunctionType.Copy
+TANH = mybir.ActivationFunctionType.Tanh
+MAX = mybir.AluOpType.max
+
+P = 128
+PACK = 4
+PASSES = K // (P * PACK)
+HALF = 512
+HALVES = S // HALF
+N_TILES = N // P
+WY_CHUNK = 256
+QUADS = 4
+SC_ROW = 24
+PLANE_ROWS = 100
+
+
+def tile_list_branch_max_combining_kernel(
+    tc, tab_words, tab_scales, offs, wa, wb_words, wb_scales, wy, wd_words, wd_scales, by, out_0, out_1, out_2, out_3
+):
+    nc = tc.nc
+    with ExitStack() as ctx:
+        keep = ctx.enter_context(tc.tile_pool(name="keep", bufs=1))
+        psum = ctx.enter_context(tc.psum_pool(name="psum", bufs=1))
+
+        def sb(shape, dtype, name, tag=None):
+            return keep.tile(shape, dtype, name=name, tag=tag or name, align_bytes=64)
+
+        def bank(index, name):
+            return psum.tile([P, HALF], F32, name=name, tag="bank%d" % index)
+
+        def cast(engine, out, in_):
+            if engine == "scalar":
+                nc.scalar.activation(out, in_, COPY)
+            else:
+                nc.vector.tensor_copy(out, in_)
+
+        offsets = keep.tile([P, S // 16], U16, name="offsets")
+        tab_sc = sb([P, T], U8, "tab_sc")
+        wb_sc_raw = sb([P, PASSES, H], U8, "wb_sc_raw")
+        v_planes = sb([P, PASSES, S], U8, "v_planes")
+        nc.gpsimd.memset(wb_sc_raw[:].bitcast(I32), 0)
+        for q in range(QUADS):
+            nc.vector.memset(tab_sc[32 * q : 32 * q + SC_ROW, :].bitcast(I32), 0)
+        nc.gpsimd.memset(v_planes[:].bitcast(I32), 0)
+
+        def load_tab(a, tag):
+            tile = sb([P, T], I32, "tab%d" % a, tag)
+            nc.sync.dma_start(tile[:], tab_words[a].rearrange("p t i -> p (t i)").bitcast(I32))
+            return tile
+
+        def load_wa(a, tag):
+            tile = sb([P, PACK, H], F32, "wa_raw%d" % a, tag)
+            nc.sync.dma_start(tile[:], wa[512 * a : 512 * (a + 1), :].rearrange("(p j) c -> p j c", j=PACK))
+            return tile
+
+        nc.sync.dma_start(offsets[:], offs)
+        for q in range(QUADS):
+            nc.sync.dma_start(
+                tab_sc[32 * q + SC_ROW : 32 * (q + 1), :].bitcast(I32),
+                tab_scales[:, 4 * q : 4 * q + 4, :].bitcast(I32),
+            )
+        wb_raw = sb([P, PASSES, 2 * H], U8, "wb_raw")
+        nc.sync.dma_start(wb_raw[:].bitcast(I32), wb_words.rearrange("a p c -> p a c").bitcast(I32))
+        tab = [load_tab(0, "tab0")]
+        for q in range(QUADS):
+            nc.sync.dma_start(
+                wb_sc_raw[32 * q : 32 * q + 4, :, :].bitcast(I32),
+                wb_scales[:, 4 * q : 4 * q + 4, :].rearrange("a r c -> r a c").bitcast(I32),
+            )
+        tab.append(load_tab(1, "tab1"))
+
+        v_sc = sb([P, S], U8, "v_sc")
+        nc.vector.tensor_copy(v_sc[:], tab_sc[:].indirect(offsets[:]))
+        for a, queue in enumerate((nc.scalar, nc.sync)):
+            first = SC_ROW + 4 * a
+            queue.dma_start(v_planes[0:PLANE_ROWS, a, :].bitcast(I32), v_sc[first : first + PLANE_ROWS, :].bitcast(I32))
+
+        wb = sb([P, PASSES, 2 * H], U8, "wb")
+        nc.vector.tensor_copy(
+            wb[:].bitcast(U16).rearrange("p a (t m) -> p a t m", t=PACK),
+            wb_raw[:].bitcast(U16).rearrange("p a (m t) -> p a t m", t=PACK),
+        )
+        wa_raw = [load_wa(0, "wb_raw")]
+        wb_sc = sb([P, PASSES, H], U8, "wb_sc")
+        nc.vector.tensor_copy(
+            wb_sc[:].rearrange("p a (t m) -> p a t m", t=PACK),
+            wb_sc_raw[:].rearrange("p a (m t) -> p a t m", t=PACK),
+        )
+        wa_raw.append(load_wa(1, "wb_sc_raw"))
+
+        v = {}
+        for a in range(PASSES):
+            for s in range(HALVES):
+                v[a, s] = sb([P, HALF], U32, "v%d_%d" % (a, s))
+                cols = HALF // 16
+                nc.vector.tensor_copy(v[a, s][:], tab[a][:].bitcast(U32).indirect(offsets[:, cols * s : cols * (s + 1)]))
+        wy_raw = sb([P, PACK, N], F32, "wy_raw", "tab0")
+        nc.sync.dma_start(wy_raw[:], wy.rearrange("(p j) n -> p j n", j=PACK))
+        wd = sb([P, PASSES, N], I32, "wd", "tab1")
+        nc.sync.dma_start(wd[:], wd_words.rearrange("a p c i -> p a (c i)").bitcast(I32))
+
+        def times_v(acc, lhsT, lhsT_scale, a, s, start, stop):
+            nc.tensor.matmul_mx(
+                out=acc[:],
+                lhsT=lhsT,
+                lhsT_scale=lhsT_scale,
+                rhs=v[a, s][:].bitcast(FP8X4),
+                rhs_scale=v_planes[:, a, HALF * s : HALF * (s + 1)],
+                start=start,
+                stop=stop,
+            )
+
+        def branch_b(acc, a, s, t):
+            times_v(
+                acc,
+                wb[:, a, 2 * P * t : 2 * P * (t + 1)].bitcast(FP4X4),
+                wb_sc[:, a, P * t : P * (t + 1)],
+                a, s, a == 0, a == PASSES - 1,
+            )
+
+        def branch_a(acc, a, s, t):
+            cols = slice(P * t, P * (t + 1))
+            times_v(acc, wa_q[:, a, cols].bitcast(FP8X4), wa_sc[:, a, cols], a, s, a == 0, a == PASSES - 1)
+
+        b_acc = {(s, t): bank(PACK * s + t, "b_acc%d_%d" % (s, t)) for s in range(HALVES) for t in range(PACK)}
+        for a in range(PASSES):
+            for s in range(HALVES):
+                for t in range(PACK):
+                    branch_b(b_acc[s, t], a, s, t)
+
+        wa_q = sb([P, PASSES, H], U32, "wa_q")
+        wa_sc = sb([P, PASSES, H], U8, "wa_sc")
+        wa_bf = {}
+        wa_engine = ["scalar", "vector"]
+        for a in range(PASSES):
+            for u in range(2):
+                wa_bf[a, u] = sb([P, 2 * P * PACK], BF16, "wa_bf%d_%d" % (a, u))
+                cast(
+                    wa_engine[(a + u) % 2],
+                    wa_bf[a, u][:].rearrange("p (t m j) -> p m j t", t=2, j=PACK),
+                    wa_raw[a][:].rearrange("p j (m t) -> p m j t", t=PACK)[:, :, :, 2 * u : 2 * u + 2],
+                )
+            for u in range(2):
+                cols = slice(2 * P * u, 2 * P * (u + 1))
+                nc.vector.quantize_mx(out=wa_q[:, a, cols].bitcast(FP8X4), scales=wa_sc[:, a, cols], in_=wa_bf[a, u][:])
+        wd_sc = sb([P, PASSES, N], U8, "wd_sc", "wa_bf0_1")
+        nc.gpsimd.memset(wd_sc[:].bitcast(I32), 0)
+        for q in range(QUADS):
+            nc.sync.dma_start(
+                wd_sc[32 * q : 32 * q + 4, :, :].bitcast(I32),
+                wd_scales[:, 4 * q : 4 * q + 4, :].rearrange("a r c -> r a c").bitcast(I32),
+            )
+        bias = sb([P, N_TILES], F32, "bias", "wb_raw")
+        with nc.allow_non_contiguous_dma(reason="one bias value for each output row"):
+            nc.sync.dma_start(bias[:], by.rearrange("(c p) -> p c", p=P))
+
+        b_sb = [sb([P, PACK, HALF], F32, "b_sb%d" % s) for s in range(HALVES)]
+        a_acc = {}
+        for s in range(HALVES):
+            for t in range(PACK):
+                nc.scalar.activation(b_sb[s][:, t, :], b_acc[s, t][:], COPY)
+        for s in range(HALVES):
+            a_acc[s] = [bank(PACK * s + t, "a_acc%d_%d" % (s, t)) for t in range(PACK)]
+            for t in range(PACK):
+                for a in range(PASSES):
+                    branch_a(a_acc[s][t], a, s, t)
+
+        wy_q = sb([P, N], U32, "wy_q")
+        wy_sc = sb([P, N], U8, "wy_sc")
+        wy_bf = []
+        for c in range(N // WY_CHUNK):
+            wy_bf.append(sb([P, WY_CHUNK * PACK], BF16, "wy_bf%d" % c))
+            cast(
+                "scalar",
+                wy_bf[c][:].rearrange("p (c i j) -> p c j i", i=4, j=PACK),
+                wy_raw[:, :, WY_CHUNK * c : WY_CHUNK * (c + 1)].rearrange("p j (c i) -> p c j i", i=4),
+            )
+
+        def quantize_wy(c):
+            cols = slice(WY_CHUNK * c, WY_CHUNK * (c + 1))
+            nc.vector.quantize_mx(out=wy_q[:, cols].bitcast(FP8X4), scales=wy_sc[:, cols], in_=wy_bf[c][:])
+
+        h = [sb([P, PACK, HALF], F32, "h%d" % s) for s in range(HALVES)]
+        h_bf = [sb([P, HALF * PACK], BF16, "h_bf%d" % s) for s in range(HALVES)]
+        h_q = sb([P, S], U32, "h_q")
+        h_sc = sb([P, S], U8, "h_sc")
+        h_out = out_1.rearrange("(p t) j -> p t j", t=PACK)
+        words_out = out_2[0].rearrange("p m t -> p (m t)").bitcast(I32)
+
+        def combine(s):
+            tokens = slice(HALF * s, HALF * (s + 1))
+            for t in range(PACK):
+                nc.vector.tensor_tensor(h[s][:, t, :], a_acc[s][t][:], b_sb[s][:, t, :], MAX)
+                nc.sync.dma_start(h_out[:, t, tokens], h[s][:, t, :])
+            nc.vector.tensor_copy(
+                h_bf[s][:].rearrange("p (c i t) -> p c t i", i=4, t=PACK),
+                h[s][:].rearrange("p t (c i) -> p c t i", i=4),
+            )
+            nc.vector.quantize_mx(out=h_q[:, tokens].bitcast(FP8X4), scales=h_sc[:, tokens], in_=h_bf[s][:])
+            nc.sync.dma_start(words_out[:, tokens], h_q[:, tokens].bitcast(I32))
+
+        y = {}
+
+        def direct(s, n):
+            cols = slice(P * n, P * (n + 1))
+            y[s, n] = bank((N_TILES * s + n) % 8, "y_acc%d_%d" % (s, n))
+            for a in range(PASSES):
+                times_v(y[s, n], wd[:, a, cols].bitcast(FP8X4), wd_sc[:, a, cols], a, s, a == 0, False)
+
+        def detect(s, n):
+            cols = slice(P * n, P * (n + 1))
+            tokens = slice(HALF * s, HALF * (s + 1))
+            nc.tensor.matmul_mx(
+                out=y[s, n][:],
+                lhsT=wy_q[:, cols].bitcast(FP8X4),
+                lhsT_scale=wy_sc[:, cols],
+                rhs=h_q[:, tokens].bitcast(FP8X4),
+                rhs_scale=h_sc[:, tokens],
+                start=False,
+                stop=True,
+            )
+            res = sb([P, HALF], F32, "y%d_%d" % (s, n))
+            nc.scalar.activation(res[:], y[s, n][:], TANH, bias=bias[:, n : n + 1])
+            nc.sync.dma_start(out_0[cols, tokens], res[:])
+
+        for c in range(N // WY_CHUNK):
+            quantize_wy(c)
+        combine(0)
+        combine(1)
+        for q in range(QUADS):
+            nc.sync.dma_start(out_3[0, 4 * q : 4 * q + 4, :].bitcast(I32), h_sc[32 * q : 32 * q + 4, :].bitcast(I32))
+        for n in range(4):
+            direct(0, n)
+        for n in range(4):
+            detect(0, n)
+        for n in range(4, N_TILES):
+            direct(0, n)
+            detect(0, n)
+        for n in range(N_TILES):
+            direct(1, n)
+            detect(1, n)

@@ -25,8 +25,8 @@ HALVES = S // HALF
 N_TILES = N // P
 WY_CHUNK = 256
 QUADS = 4
-SC_ROW = 24
-PLANE_ROWS = 100
+SC_ROW = 96
+WB_COL, WD_COL, SC_COLS = S, S + H, S + H + N
 
 
 def tile_list_branch_max_combining_kernel(
@@ -51,12 +51,12 @@ def tile_list_branch_max_combining_kernel(
 
         offsets = keep.tile([P, S // 16], U16, name="offsets")
         tab_sc = sb([P, T], U8, "tab_sc")
-        wb_sc_raw = sb([P, PASSES, H], U8, "wb_sc_raw")
-        v_planes = sb([P, PASSES, S], U8, "v_planes")
-        nc.gpsimd.memset(wb_sc_raw[:].bitcast(I32), 0)
-        for q in range(QUADS):
-            nc.vector.memset(tab_sc[32 * q : 32 * q + SC_ROW, :].bitcast(I32), 0)
-        nc.gpsimd.memset(v_planes[:].bitcast(I32), 0)
+        wb_sc_raw = sb([P, H], U8, "wb_sc_raw")
+        sc_rows = sb([P, SC_COLS], U8, "sc_rows")
+        planes = sb([P, PASSES, SC_COLS], U8, "planes")
+        nc.vector.memset(wb_sc_raw[0:SC_ROW, :].bitcast(I32), 0)
+        nc.vector.memset(tab_sc[0:SC_ROW, :].bitcast(I32), 0)
+        nc.gpsimd.memset(planes[:].bitcast(I32), 0)
 
         def load_tab(a, tag):
             tile = sb([P, T], I32, "tab%d" % a, tag)
@@ -68,40 +68,36 @@ def tile_list_branch_max_combining_kernel(
             nc.sync.dma_start(tile[:], wa[512 * a : 512 * (a + 1), :].rearrange("(p j) c -> p j c", j=PACK))
             return tile
 
+        def load_scale_rows(tile, scales):
+            nc.sync.dma_start(tile[SC_ROW:P].bitcast(I32), scales.rearrange("a q c -> (a q) c").bitcast(I32))
+
         nc.sync.dma_start(offsets[:], offs)
-        for q in range(QUADS):
-            nc.sync.dma_start(
-                tab_sc[32 * q + SC_ROW : 32 * (q + 1), :].bitcast(I32),
-                tab_scales[:, 4 * q : 4 * q + 4, :].bitcast(I32),
-            )
+        load_scale_rows(wb_sc_raw[:], wb_scales)
+        load_scale_rows(tab_sc[:], tab_scales)
+        load_scale_rows(sc_rows[:, WD_COL:SC_COLS], wd_scales)
         wb_raw = sb([P, PASSES, 2 * H], U8, "wb_raw")
         nc.sync.dma_start(wb_raw[:].bitcast(I32), wb_words.rearrange("a p c -> p a c").bitcast(I32))
-        tab = [load_tab(0, "tab0")]
-        for q in range(QUADS):
-            nc.sync.dma_start(
-                wb_sc_raw[32 * q : 32 * q + 4, :, :].bitcast(I32),
-                wb_scales[:, 4 * q : 4 * q + 4, :].rearrange("a r c -> r a c").bitcast(I32),
-            )
-        tab.append(load_tab(1, "tab1"))
+        tab = [load_tab(a, "tab%d" % a) for a in range(PASSES)]
 
+        nc.vector.tensor_copy(
+            sc_rows[:, WB_COL:WD_COL].rearrange("p (t m) -> p t m", t=PACK),
+            wb_sc_raw[:].rearrange("p (m t) -> p t m", t=PACK),
+        )
         v_sc = sb([P, S], U8, "v_sc")
         nc.vector.tensor_copy(v_sc[:], tab_sc[:].indirect(offsets[:]))
-        for a, queue in enumerate((nc.scalar, nc.sync)):
-            first = SC_ROW + 4 * a
-            queue.dma_start(v_planes[0:PLANE_ROWS, a, :].bitcast(I32), v_sc[first : first + PLANE_ROWS, :].bitcast(I32))
+        nc.vector.tensor_copy(sc_rows[SC_ROW:P, 0:S].bitcast(I32), v_sc[SC_ROW:P, :].bitcast(I32))
+        for a, queue in enumerate((nc.scalar, nc.scalar)):
+            for q in range(QUADS):
+                row = SC_ROW + 16 * a + 4 * q
+                queue.dma_start(planes[32 * q : 32 * q + 4, a, :].bitcast(I32), sc_rows[row : row + 4, :].bitcast(I32))
+        wa_raw = [load_wa(0, "tab_sc")]
 
-        wb = sb([P, PASSES, 2 * H], U8, "wb")
+        wb = sb([P, PASSES, 2 * H], U8, "wb", "v_sc")
         nc.vector.tensor_copy(
             wb[:].bitcast(U16).rearrange("p a (t m) -> p a t m", t=PACK),
             wb_raw[:].bitcast(U16).rearrange("p a (m t) -> p a t m", t=PACK),
         )
-        wa_raw = [load_wa(0, "wb_raw")]
-        wb_sc = sb([P, PASSES, H], U8, "wb_sc")
-        nc.vector.tensor_copy(
-            wb_sc[:].rearrange("p a (t m) -> p a t m", t=PACK),
-            wb_sc_raw[:].rearrange("p a (m t) -> p a t m", t=PACK),
-        )
-        wa_raw.append(load_wa(1, "wb_sc_raw"))
+        wa_raw.append(load_wa(1, "wb_raw"))
 
         v = {}
         for a in range(PASSES):
@@ -109,10 +105,10 @@ def tile_list_branch_max_combining_kernel(
                 v[a, s] = sb([P, HALF], U32, "v%d_%d" % (a, s))
                 cols = HALF // 16
                 nc.vector.tensor_copy(v[a, s][:], tab[a][:].bitcast(U32).indirect(offsets[:, cols * s : cols * (s + 1)]))
-        wy_raw = sb([P, PACK, N], F32, "wy_raw", "tab0")
-        nc.sync.dma_start(wy_raw[:], wy.rearrange("(p j) n -> p j n", j=PACK))
-        wd = sb([P, PASSES, N], I32, "wd", "tab1")
+        wd = sb([P, PASSES, N], I32, "wd", "tab0")
         nc.sync.dma_start(wd[:], wd_words.rearrange("a p c i -> p a (c i)").bitcast(I32))
+        wy_raw = sb([P, PACK, N], F32, "wy_raw", "tab1")
+        nc.sync.dma_start(wy_raw[:], wy.rearrange("(p j) n -> p j n", j=PACK))
 
         def times_v(acc, lhsT, lhsT_scale, a, s, start, stop):
             nc.tensor.matmul_mx(
@@ -120,7 +116,7 @@ def tile_list_branch_max_combining_kernel(
                 lhsT=lhsT,
                 lhsT_scale=lhsT_scale,
                 rhs=v[a, s][:].bitcast(FP8X4),
-                rhs_scale=v_planes[:, a, HALF * s : HALF * (s + 1)],
+                rhs_scale=planes[:, a, HALF * s : HALF * (s + 1)],
                 start=start,
                 stop=stop,
             )
@@ -129,7 +125,7 @@ def tile_list_branch_max_combining_kernel(
             times_v(
                 acc,
                 wb[:, a, 2 * P * t : 2 * P * (t + 1)].bitcast(FP4X4),
-                wb_sc[:, a, P * t : P * (t + 1)],
+                planes[:, a, WB_COL + P * t : WB_COL + P * (t + 1)],
                 a, s, a == 0, a == PASSES - 1,
             )
 
@@ -146,26 +142,18 @@ def tile_list_branch_max_combining_kernel(
         wa_q = sb([P, PASSES, H], U32, "wa_q")
         wa_sc = sb([P, PASSES, H], U8, "wa_sc")
         wa_bf = {}
-        wa_engine = ["scalar", "vector"]
         for a in range(PASSES):
             for u in range(2):
                 wa_bf[a, u] = sb([P, 2 * P * PACK], BF16, "wa_bf%d_%d" % (a, u))
                 cast(
-                    wa_engine[(a + u) % 2],
+                    "vector",
                     wa_bf[a, u][:].rearrange("p (t m j) -> p m j t", t=2, j=PACK),
                     wa_raw[a][:].rearrange("p j (m t) -> p m j t", t=PACK)[:, :, :, 2 * u : 2 * u + 2],
                 )
             for u in range(2):
                 cols = slice(2 * P * u, 2 * P * (u + 1))
                 nc.vector.quantize_mx(out=wa_q[:, a, cols].bitcast(FP8X4), scales=wa_sc[:, a, cols], in_=wa_bf[a, u][:])
-        wd_sc = sb([P, PASSES, N], U8, "wd_sc", "wa_bf0_1")
-        nc.gpsimd.memset(wd_sc[:].bitcast(I32), 0)
-        for q in range(QUADS):
-            nc.sync.dma_start(
-                wd_sc[32 * q : 32 * q + 4, :, :].bitcast(I32),
-                wd_scales[:, 4 * q : 4 * q + 4, :].rearrange("a r c -> r a c").bitcast(I32),
-            )
-        bias = sb([P, N_TILES], F32, "bias", "wb_raw")
+        bias = sb([P, N_TILES], F32, "bias", "wa_bf0_0")
         with nc.allow_non_contiguous_dma(reason="one bias value for each output row"):
             nc.sync.dma_start(bias[:], by.rearrange("(c p) -> p c", p=P))
 
@@ -174,19 +162,20 @@ def tile_list_branch_max_combining_kernel(
         for s in range(HALVES):
             for t in range(PACK):
                 nc.scalar.activation(b_sb[s][:, t, :], b_acc[s, t][:], COPY)
-        for s in range(HALVES):
-            a_acc[s] = [bank(PACK * s + t, "a_acc%d_%d" % (s, t)) for t in range(PACK)]
+
+        def multiply_a(s):
+            a_acc[s] = [bank(t, "a_acc%d_%d" % (s, t)) for t in range(PACK)]
             for t in range(PACK):
                 for a in range(PASSES):
                     branch_a(a_acc[s][t], a, s, t)
 
         wy_q = sb([P, N], U32, "wy_q")
         wy_sc = sb([P, N], U8, "wy_sc")
-        wy_bf = []
-        for c in range(N // WY_CHUNK):
-            wy_bf.append(sb([P, WY_CHUNK * PACK], BF16, "wy_bf%d" % c))
+        wy_bf = [sb([P, WY_CHUNK * PACK], BF16, "wy_bf%d" % c) for c in range(N // WY_CHUNK)]
+
+        def round_wy(c, engine):
             cast(
-                "scalar",
+                engine,
                 wy_bf[c][:].rearrange("p (c i j) -> p c j i", i=4, j=PACK),
                 wy_raw[:, :, WY_CHUNK * c : WY_CHUNK * (c + 1)].rearrange("p j (c i) -> p c j i", i=4),
             )
@@ -207,10 +196,19 @@ def tile_list_branch_max_combining_kernel(
             for t in range(PACK):
                 nc.vector.tensor_tensor(h[s][:, t, :], a_acc[s][t][:], b_sb[s][:, t, :], MAX)
                 nc.sync.dma_start(h_out[:, t, tokens], h[s][:, t, :])
-            nc.vector.tensor_copy(
-                h_bf[s][:].rearrange("p (c i t) -> p c t i", i=4, t=PACK),
-                h[s][:].rearrange("p t (c i) -> p c t i", i=4),
-            )
+
+        def round_h(s, engine):
+            cut = (128, 128)[s]
+            for eng, lo, hi in (("scalar", 0, cut), ("vector", cut, HALF)):
+                if hi > lo:
+                    cast(
+                        eng,
+                        h_bf[s][:, PACK * lo : PACK * hi].rearrange("p (c i t) -> p c t i", i=4, t=PACK),
+                        h[s][:, :, lo:hi].rearrange("p t (c i) -> p c t i", i=4),
+                    )
+
+        def quantize_h(s):
+            tokens = slice(HALF * s, HALF * (s + 1))
             nc.vector.quantize_mx(out=h_q[:, tokens].bitcast(FP8X4), scales=h_sc[:, tokens], in_=h_bf[s][:])
             nc.sync.dma_start(words_out[:, tokens], h_q[:, tokens].bitcast(I32))
 
@@ -218,9 +216,9 @@ def tile_list_branch_max_combining_kernel(
 
         def direct(s, n):
             cols = slice(P * n, P * (n + 1))
-            y[s, n] = bank((N_TILES * s + n) % 8, "y_acc%d_%d" % (s, n))
+            y[s, n] = bank((PACK + N_TILES * s + n) % 8, "y_acc%d_%d" % (s, n))
             for a in range(PASSES):
-                times_v(y[s, n], wd[:, a, cols].bitcast(FP8X4), wd_sc[:, a, cols], a, s, a == 0, False)
+                times_v(y[s, n], wd[:, a, cols].bitcast(FP8X4), planes[:, a, WD_COL + P * n : WD_COL + P * (n + 1)], a, s, a == 0, False)
 
         def detect(s, n):
             cols = slice(P * n, P * (n + 1))
@@ -238,16 +236,25 @@ def tile_list_branch_max_combining_kernel(
             nc.scalar.activation(res[:], y[s, n][:], TANH, bias=bias[:, n : n + 1])
             nc.sync.dma_start(out_0[cols, tokens], res[:])
 
-        for c in range(N // WY_CHUNK):
-            quantize_wy(c)
+        multiply_a(0)
         combine(0)
-        combine(1)
-        for q in range(QUADS):
-            nc.sync.dma_start(out_3[0, 4 * q : 4 * q + 4, :].bitcast(I32), h_sc[32 * q : 32 * q + 4, :].bitcast(I32))
+        round_h(0, "vector")
+        quantize_h(0)
+        round_wy(0, "scalar")
+        quantize_wy(0)
+        round_wy(1, "scalar")
+        quantize_wy(1)
         for n in range(4):
             direct(0, n)
-        for n in range(4):
             detect(0, n)
+        multiply_a(1)
+        combine(1)
+        round_wy(2, "scalar")
+        quantize_wy(2)
+        round_h(1, "vector")
+        quantize_h(1)
+        for q in range(QUADS):
+            nc.gpsimd.dma_start(out_3[0, 4 * q : 4 * q + 4, :].bitcast(I32), h_sc[32 * q : 32 * q + 4, :].bitcast(I32))
         for n in range(4, N_TILES):
             direct(0, n)
             detect(0, n)

@@ -75,8 +75,9 @@ def tile_list_branch_max_combining_kernel(
         load_scale_rows(wb_sc_raw[:], wb_scales)
         load_scale_rows(tab_sc[:], tab_scales)
         load_scale_rows(sc_rows[:, WD_COL:SC_COLS], wd_scales)
-        wb_raw = sb([P, PASSES, 2 * H], U8, "wb_raw")
-        nc.sync.dma_start(wb_raw[:].bitcast(I32), wb_words.rearrange("a p c -> p a c").bitcast(I32))
+        wb_raw = [sb([P, 2 * H], U8, "wb_raw%d" % a) for a in range(PASSES)]
+        for a in range(PASSES):
+            nc.sync.dma_start(wb_raw[a][:].bitcast(I32), wb_words[a].bitcast(I32))
         tab = [load_tab(a, "tab%d" % a) for a in range(PASSES)]
 
         nc.vector.tensor_copy(
@@ -90,14 +91,15 @@ def tile_list_branch_max_combining_kernel(
             for q in range(QUADS):
                 row = SC_ROW + 16 * a + 4 * q
                 queue.dma_start(planes[32 * q : 32 * q + 4, a, :].bitcast(I32), sc_rows[row : row + 4, :].bitcast(I32))
-        wa_raw = [load_wa(0, "tab_sc")]
 
         wb = sb([P, PASSES, 2 * H], U8, "wb", "v_sc")
-        nc.vector.tensor_copy(
-            wb[:].bitcast(U16).rearrange("p a (t m) -> p a t m", t=PACK),
-            wb_raw[:].bitcast(U16).rearrange("p a (m t) -> p a t m", t=PACK),
-        )
-        wa_raw.append(load_wa(1, "wb_raw"))
+        wa_raw = []
+        for a in range(PASSES):
+            nc.vector.tensor_copy(
+                wb[:, a, :].bitcast(U16).rearrange("p (t m) -> p t m", t=PACK),
+                wb_raw[a][:].bitcast(U16).rearrange("p (m t) -> p t m", t=PACK),
+            )
+            wa_raw.append(load_wa(a, "wb_raw%d" % a))
 
         v = {}
         for a in range(PASSES):
@@ -105,18 +107,18 @@ def tile_list_branch_max_combining_kernel(
                 v[a, s] = sb([P, HALF], U32, "v%d_%d" % (a, s))
                 cols = HALF // 16
                 nc.vector.tensor_copy(v[a, s][:], tab[a][:].bitcast(U32).indirect(offsets[:, cols * s : cols * (s + 1)]))
-        wd = sb([P, PASSES, N], I32, "wd", "tab0")
-        nc.sync.dma_start(wd[:], wd_words.rearrange("a p c i -> p a (c i)").bitcast(I32))
-        wy_raw = sb([P, PACK, N], F32, "wy_raw", "tab1")
+        wy_raw = sb([P, PACK, N], F32, "wy_raw", "tab0")
         nc.sync.dma_start(wy_raw[:], wy.rearrange("(p j) n -> p j n", j=PACK))
+        wd = sb([P, PASSES, N], I32, "wd", "tab1")
+        nc.sync.dma_start(wd[:], wd_words.rearrange("a p c i -> p a (c i)").bitcast(I32))
 
-        def times_v(acc, lhsT, lhsT_scale, a, s, start, stop):
+        def times_v(acc, lhsT, lhsT_scale, a, s, start, stop, lo=0, hi=HALF):
             nc.tensor.matmul_mx(
-                out=acc[:],
+                out=acc[:, 0 : hi - lo],
                 lhsT=lhsT,
                 lhsT_scale=lhsT_scale,
-                rhs=v[a, s][:].bitcast(FP8X4),
-                rhs_scale=planes[:, a, HALF * s : HALF * (s + 1)],
+                rhs=v[a, s][:, lo:hi].bitcast(FP8X4),
+                rhs_scale=planes[:, a, HALF * s + lo : HALF * s + hi],
                 start=start,
                 stop=stop,
             )
@@ -146,7 +148,7 @@ def tile_list_branch_max_combining_kernel(
             for u in range(2):
                 wa_bf[a, u] = sb([P, 2 * P * PACK], BF16, "wa_bf%d_%d" % (a, u))
                 cast(
-                    "vector",
+                    "scalar" if (a, u) == (0, 0) else "vector",
                     wa_bf[a, u][:].rearrange("p (t m j) -> p m j t", t=2, j=PACK),
                     wa_raw[a][:].rearrange("p j (m t) -> p m j t", t=PACK)[:, :, :, 2 * u : 2 * u + 2],
                 )
@@ -157,21 +159,20 @@ def tile_list_branch_max_combining_kernel(
         with nc.allow_non_contiguous_dma(reason="one bias value for each output row"):
             nc.sync.dma_start(bias[:], by.rearrange("(c p) -> p c", p=P))
 
-        b_sb = [sb([P, PACK, HALF], F32, "b_sb%d" % s) for s in range(HALVES)]
+        b_sb = [sb([P, PACK, HALF], F32, "b_sb%d" % s, tag) for s, tag in enumerate(("wb_raw0", "b_sb1"))]
         a_acc = {}
         for s in range(HALVES):
             for t in range(PACK):
                 nc.scalar.activation(b_sb[s][:, t, :], b_acc[s, t][:], COPY)
 
         def multiply_a(s):
-            a_acc[s] = [bank(t, "a_acc%d_%d" % (s, t)) for t in range(PACK)]
+            a_acc[s] = [bank(PACK * s + t, "a_acc%d_%d" % (s, t)) for t in range(PACK)]
             for t in range(PACK):
                 for a in range(PASSES):
                     branch_a(a_acc[s][t], a, s, t)
 
         wy_q = sb([P, N], U32, "wy_q")
         wy_sc = sb([P, N], U8, "wy_sc")
-        wy_bf = [sb([P, WY_CHUNK * PACK], BF16, "wy_bf%d" % c) for c in range(N // WY_CHUNK)]
 
         def round_wy(c, engine):
             cast(
@@ -197,7 +198,7 @@ def tile_list_branch_max_combining_kernel(
                 nc.vector.tensor_tensor(h[s][:, t, :], a_acc[s][t][:], b_sb[s][:, t, :], MAX)
                 nc.sync.dma_start(h_out[:, t, tokens], h[s][:, t, :])
 
-        def round_h(s, engine):
+        def round_h(s):
             cut = (128, 128)[s]
             for eng, lo, hi in (("scalar", 0, cut), ("vector", cut, HALF)):
                 if hi > lo:
@@ -212,19 +213,21 @@ def tile_list_branch_max_combining_kernel(
             nc.vector.quantize_mx(out=h_q[:, tokens].bitcast(FP8X4), scales=h_sc[:, tokens], in_=h_bf[s][:])
             nc.sync.dma_start(words_out[:, tokens], h_q[:, tokens].bitcast(I32))
 
-        y = {}
+        y_acc = {}
 
-        def direct(s, n):
+        def direct(index, s, n, lo, hi):
             cols = slice(P * n, P * (n + 1))
-            y[s, n] = bank((PACK + N_TILES * s + n) % 8, "y_acc%d_%d" % (s, n))
+            y_acc[index] = bank(index % 8, "y_acc%d" % index)
             for a in range(PASSES):
-                times_v(y[s, n], wd[:, a, cols].bitcast(FP8X4), planes[:, a, WD_COL + P * n : WD_COL + P * (n + 1)], a, s, a == 0, False)
+                scale = planes[:, a, WD_COL + P * n : WD_COL + P * (n + 1)]
+                times_v(y_acc[index], wd[:, a, cols].bitcast(FP8X4), scale, a, s, a == 0, False, lo, hi)
 
-        def detect(s, n):
+        def detect(index, s, n, lo, hi):
             cols = slice(P * n, P * (n + 1))
-            tokens = slice(HALF * s, HALF * (s + 1))
+            tokens = slice(HALF * s + lo, HALF * s + hi)
+            acc = y_acc[index]
             nc.tensor.matmul_mx(
-                out=y[s, n][:],
+                out=acc[:, 0 : hi - lo],
                 lhsT=wy_q[:, cols].bitcast(FP8X4),
                 lhsT_scale=wy_sc[:, cols],
                 rhs=h_q[:, tokens].bitcast(FP8X4),
@@ -232,32 +235,33 @@ def tile_list_branch_max_combining_kernel(
                 start=False,
                 stop=True,
             )
-            res = sb([P, HALF], F32, "y%d_%d" % (s, n))
-            nc.scalar.activation(res[:], y[s, n][:], TANH, bias=bias[:, n : n + 1])
+            res = sb([P, hi - lo], F32, "y%d" % index)
+            nc.scalar.activation(res[:], acc[:, 0 : hi - lo], TANH, bias=bias[:, n : n + 1])
             nc.sync.dma_start(out_0[cols, tokens], res[:])
 
         multiply_a(0)
+        multiply_a(1)
         combine(0)
-        round_h(0, "vector")
+        wy_bf_all = sb([P, N * PACK], BF16, "wy_bf", "wb_raw0")
+        wy_bf = [wy_bf_all[:, WY_CHUNK * PACK * c : WY_CHUNK * PACK * (c + 1)] for c in range(N // WY_CHUNK)]
+        round_h(0)
         quantize_h(0)
         round_wy(0, "scalar")
         quantize_wy(0)
         round_wy(1, "scalar")
         quantize_wy(1)
-        for n in range(4):
-            direct(0, n)
-            detect(0, n)
-        multiply_a(1)
         combine(1)
         round_wy(2, "scalar")
         quantize_wy(2)
-        round_h(1, "vector")
+        round_h(1)
         quantize_h(1)
         for q in range(QUADS):
             nc.gpsimd.dma_start(out_3[0, 4 * q : 4 * q + 4, :].bitcast(I32), h_sc[32 * q : 32 * q + 4, :].bitcast(I32))
-        for n in range(4, N_TILES):
-            direct(0, n)
-            detect(0, n)
-        for n in range(N_TILES):
-            direct(1, n)
-            detect(1, n)
+        pieces = [(s, n, 0, HALF) for s in range(HALVES) for n in range(N_TILES - s)]
+        pieces += [(1, N_TILES - 1, 0, HALF // 2), (1, N_TILES - 1, HALF // 2, HALF)]
+        for index in range(PACK):
+            direct(index, *pieces[index])
+        for index, piece in enumerate(pieces):
+            if index >= PACK:
+                direct(index, *piece)
+            detect(index, *piece)

@@ -1,6 +1,7 @@
 from contextlib import ExitStack
 
 import concourse.mybir as mybir
+from concourse.masks import make_identity
 
 T, S, K, H, N = 2048, 1024, 1024, 512, 768
 FLOPS = 2 * S * (2 * K * H + H * N + K * N)
@@ -25,7 +26,8 @@ HALVES = S // HALF
 N_TILES = N // P
 WY_CHUNK = 256
 QUADS = 4
-SC_ROW = 96
+SCALAR_TOKENS = 160
+SC_ROWS = 32
 WB_COL, WD_COL, SC_COLS = S, S + H, S + H + N
 
 
@@ -52,11 +54,22 @@ def tile_list_branch_max_combining_kernel(
         offsets = keep.tile([P, S // 16], U16, name="offsets")
         tab_sc = sb([P, T], U8, "tab_sc")
         wb_sc_raw = sb([P, H], U8, "wb_sc_raw")
-        sc_rows = sb([P, SC_COLS], U8, "sc_rows")
-        planes = sb([P, PASSES, SC_COLS], U8, "planes")
-        nc.vector.memset(wb_sc_raw[0:SC_ROW, :].bitcast(I32), 0)
-        nc.vector.memset(tab_sc[0:SC_ROW, :].bitcast(I32), 0)
-        nc.gpsimd.memset(planes[:].bitcast(I32), 0)
+        planes = [sb([P, SC_COLS], U8, "plane%d" % a) for a in range(PASSES)]
+        for lo, hi in ((SC_ROWS, 64), (64, P)):
+            nc.vector.memset(tab_sc[lo:hi, :].bitcast(I32), 0)
+            nc.vector.memset(wb_sc_raw[lo:hi, :].bitcast(I32), 0)
+            nc.vector.memset(planes[0][lo:hi, WD_COL:SC_COLS].bitcast(I32), 0)
+
+        by_rows = sb([P, P], F32, "by_rows")
+        nc.gpsimd.memset(by_rows[:], 0.0)
+        identity = sb([P, P], F32, "identity")
+        make_identity(nc, identity[:])
+        nc.gpsimd.memset(planes[1][:].bitcast(I32), 0)
+        nc.scalar.dma_start(by_rows[0:N_TILES, :], by.rearrange("(c p) -> c p", p=P))
+        by_cols = psum.tile([P, P], F32, name="by_cols", tag="bank7")
+        nc.tensor.transpose(by_cols[:], by_rows[:], identity[:])
+        bias = sb([P, N_TILES], F32, "bias")
+        nc.scalar.activation(bias[:], by_cols[:, 0:N_TILES], COPY)
 
         def load_tab(a, tag):
             tile = sb([P, T], I32, "tab%d" % a, tag)
@@ -69,28 +82,29 @@ def tile_list_branch_max_combining_kernel(
             return tile
 
         def load_scale_rows(tile, scales):
-            nc.sync.dma_start(tile[SC_ROW:P].bitcast(I32), scales.rearrange("a q c -> (a q) c").bitcast(I32))
+            nc.sync.dma_start(tile[0:SC_ROWS].bitcast(I32), scales.rearrange("a q c -> (a q) c").bitcast(I32))
 
         nc.sync.dma_start(offsets[:], offs)
-        load_scale_rows(wb_sc_raw[:], wb_scales)
         load_scale_rows(tab_sc[:], tab_scales)
-        load_scale_rows(sc_rows[:, WD_COL:SC_COLS], wd_scales)
+        load_scale_rows(wb_sc_raw[:], wb_scales)
+        load_scale_rows(planes[0][:, WD_COL:SC_COLS], wd_scales)
         wb_raw = [sb([P, 2 * H], U8, "wb_raw%d" % a) for a in range(PASSES)]
         for a in range(PASSES):
             nc.sync.dma_start(wb_raw[a][:].bitcast(I32), wb_words[a].bitcast(I32))
         tab = [load_tab(a, "tab%d" % a) for a in range(PASSES)]
 
         nc.vector.tensor_copy(
-            sc_rows[:, WB_COL:WD_COL].rearrange("p (t m) -> p t m", t=PACK),
+            planes[0][:, WB_COL:WD_COL].rearrange("p (t m) -> p t m", t=PACK),
             wb_sc_raw[:].rearrange("p (m t) -> p t m", t=PACK),
         )
         v_sc = sb([P, S], U8, "v_sc")
         nc.vector.tensor_copy(v_sc[:], tab_sc[:].indirect(offsets[:]))
-        nc.vector.tensor_copy(sc_rows[SC_ROW:P, 0:S].bitcast(I32), v_sc[SC_ROW:P, :].bitcast(I32))
-        for a, queue in enumerate((nc.scalar, nc.scalar)):
+        nc.vector.tensor_copy(planes[0][:, 0:S].bitcast(I32), v_sc[:].bitcast(I32))
+        for a in range(PASSES):
             for q in range(QUADS):
-                row = SC_ROW + 16 * a + 4 * q
-                queue.dma_start(planes[32 * q : 32 * q + 4, a, :].bitcast(I32), sc_rows[row : row + 4, :].bitcast(I32))
+                row = 16 * a + 4 * q
+                if row > 0:
+                    nc.scalar.dma_start(planes[a][32 * q : 32 * q + 4, :].bitcast(I32), planes[0][row : row + 4, :].bitcast(I32))
 
         wb = sb([P, PASSES, 2 * H], U8, "wb", "v_sc")
         wa_raw = []
@@ -110,7 +124,8 @@ def tile_list_branch_max_combining_kernel(
         wy_raw = sb([P, PACK, N], F32, "wy_raw", "tab0")
         nc.sync.dma_start(wy_raw[:], wy.rearrange("(p j) n -> p j n", j=PACK))
         wd = sb([P, PASSES, N], I32, "wd", "tab1")
-        nc.sync.dma_start(wd[:], wd_words.rearrange("a p c i -> p a (c i)").bitcast(I32))
+        for a in range(PASSES):
+            nc.sync.dma_start(wd[:, a, :], wd_words[a].rearrange("p c i -> p (c i)").bitcast(I32))
 
         def times_v(acc, lhsT, lhsT_scale, a, s, start, stop, lo=0, hi=HALF):
             nc.tensor.matmul_mx(
@@ -118,7 +133,7 @@ def tile_list_branch_max_combining_kernel(
                 lhsT=lhsT,
                 lhsT_scale=lhsT_scale,
                 rhs=v[a, s][:, lo:hi].bitcast(FP8X4),
-                rhs_scale=planes[:, a, HALF * s + lo : HALF * s + hi],
+                rhs_scale=planes[a][:, HALF * s + lo : HALF * s + hi],
                 start=start,
                 stop=stop,
             )
@@ -127,7 +142,7 @@ def tile_list_branch_max_combining_kernel(
             times_v(
                 acc,
                 wb[:, a, 2 * P * t : 2 * P * (t + 1)].bitcast(FP4X4),
-                planes[:, a, WB_COL + P * t : WB_COL + P * (t + 1)],
+                planes[a][:, WB_COL + P * t : WB_COL + P * (t + 1)],
                 a, s, a == 0, a == PASSES - 1,
             )
 
@@ -136,10 +151,10 @@ def tile_list_branch_max_combining_kernel(
             times_v(acc, wa_q[:, a, cols].bitcast(FP8X4), wa_sc[:, a, cols], a, s, a == 0, a == PASSES - 1)
 
         b_acc = {(s, t): bank(PACK * s + t, "b_acc%d_%d" % (s, t)) for s in range(HALVES) for t in range(PACK)}
+        groups = [(s, t) for s in range(HALVES) for t in range(PACK)]
         for a in range(PASSES):
-            for s in range(HALVES):
-                for t in range(PACK):
-                    branch_b(b_acc[s, t], a, s, t)
+            for s, t in groups:
+                branch_b(b_acc[s, t], a, s, t)
 
         wa_q = sb([P, PASSES, H], U32, "wa_q")
         wa_sc = sb([P, PASSES, H], U8, "wa_sc")
@@ -155,79 +170,86 @@ def tile_list_branch_max_combining_kernel(
             for u in range(2):
                 cols = slice(2 * P * u, 2 * P * (u + 1))
                 nc.vector.quantize_mx(out=wa_q[:, a, cols].bitcast(FP8X4), scales=wa_sc[:, a, cols], in_=wa_bf[a, u][:])
-        bias = sb([P, N_TILES], F32, "bias", "wa_bf0_0")
-        with nc.allow_non_contiguous_dma(reason="one bias value for each output row"):
-            nc.sync.dma_start(bias[:], by.rearrange("(c p) -> p c", p=P))
 
-        b_sb = [sb([P, PACK, HALF], F32, "b_sb%d" % s, tag) for s, tag in enumerate(("wb_raw0", "b_sb1"))]
-        a_acc = {}
-        for s in range(HALVES):
-            for t in range(PACK):
-                nc.scalar.activation(b_sb[s][:, t, :], b_acc[s, t][:], COPY)
+        b_tiles = [sb([P, PACK, HALF], F32, "b_sb%d" % u, "wb_raw%d" % u) for u in range(2)]
+        b_sb = {}
+        for index, (s, t) in enumerate(groups):
+            b_sb[s, t] = b_tiles[index // PACK][:, index % PACK, :]
+            nc.scalar.activation(b_sb[s, t], b_acc[s, t][:], COPY)
 
-        def multiply_a(s):
-            a_acc[s] = [bank(PACK * s + t, "a_acc%d_%d" % (s, t)) for t in range(PACK)]
+        h = sb([P, PACK, S], F32, "h")
+        h_out = out_1.rearrange("(p t) j -> p t j", t=PACK)
+
+        def combine(s):
+            tokens = slice(HALF * s, HALF * (s + 1))
             for t in range(PACK):
+                a_acc = bank(t, "a_acc%d_%d" % (s, t))
                 for a in range(PASSES):
-                    branch_a(a_acc[s][t], a, s, t)
+                    branch_a(a_acc, a, s, t)
+                nc.vector.tensor_tensor(h[:, t, tokens], a_acc[:], b_sb[s, t], MAX)
+                nc.sync.dma_start(h_out[:, t, tokens], h[:, t, tokens])
 
         wy_q = sb([P, N], U32, "wy_q")
         wy_sc = sb([P, N], U8, "wy_sc")
+        wy_bf = {}
 
-        def round_wy(c, engine):
+        def round_wy(engine, c, tag):
+            wy_bf[c] = sb([P, WY_CHUNK * PACK], BF16, "wy_bf%d" % c, tag)[:]
             cast(
                 engine,
-                wy_bf[c][:].rearrange("p (c i j) -> p c j i", i=4, j=PACK),
+                wy_bf[c].rearrange("p (c i j) -> p c j i", i=4, j=PACK),
                 wy_raw[:, :, WY_CHUNK * c : WY_CHUNK * (c + 1)].rearrange("p j (c i) -> p c j i", i=4),
             )
 
         def quantize_wy(c):
             cols = slice(WY_CHUNK * c, WY_CHUNK * (c + 1))
-            nc.vector.quantize_mx(out=wy_q[:, cols].bitcast(FP8X4), scales=wy_sc[:, cols], in_=wy_bf[c][:])
+            nc.vector.quantize_mx(out=wy_q[:, cols].bitcast(FP8X4), scales=wy_sc[:, cols], in_=wy_bf[c])
 
-        h = [sb([P, PACK, HALF], F32, "h%d" % s) for s in range(HALVES)]
-        h_bf = [sb([P, HALF * PACK], BF16, "h_bf%d" % s) for s in range(HALVES)]
+        h_bf = [sb([P, HALF * PACK], BF16, "h_bf%d" % s, "h_bf") for s in range(HALVES)]
         h_q = sb([P, S], U32, "h_q")
         h_sc = sb([P, S], U8, "h_sc")
-        h_out = out_1.rearrange("(p t) j -> p t j", t=PACK)
         words_out = out_2[0].rearrange("p m t -> p (m t)").bitcast(I32)
 
-        def combine(s):
-            tokens = slice(HALF * s, HALF * (s + 1))
-            for t in range(PACK):
-                nc.vector.tensor_tensor(h[s][:, t, :], a_acc[s][t][:], b_sb[s][:, t, :], MAX)
-                nc.sync.dma_start(h_out[:, t, tokens], h[s][:, t, :])
-
-        def round_h(s):
-            cut = (128, 128)[s]
-            for eng, lo, hi in (("scalar", 0, cut), ("vector", cut, HALF)):
-                if hi > lo:
-                    cast(
-                        eng,
-                        h_bf[s][:, PACK * lo : PACK * hi].rearrange("p (c i t) -> p c t i", i=4, t=PACK),
-                        h[s][:, :, lo:hi].rearrange("p t (c i) -> p c t i", i=4),
-                    )
+        def round_h(engine, s, lo, hi):
+            cast(
+                engine,
+                h_bf[s][:, PACK * lo : PACK * hi].rearrange("p (c i t) -> p c t i", i=4, t=PACK),
+                h[:, :, HALF * s + lo : HALF * s + hi].rearrange("p t (c i) -> p c t i", i=4),
+            )
 
         def quantize_h(s):
             tokens = slice(HALF * s, HALF * (s + 1))
             nc.vector.quantize_mx(out=h_q[:, tokens].bitcast(FP8X4), scales=h_sc[:, tokens], in_=h_bf[s][:])
             nc.sync.dma_start(words_out[:, tokens], h_q[:, tokens].bitcast(I32))
 
-        y_acc = {}
+        combine(0)
+        round_wy("scalar", 0, "wy_bf0")
+        round_h("scalar", 0, 0, SCALAR_TOKENS)
+        round_h("vector", 0, SCALAR_TOKENS, HALF)
+        quantize_wy(0)
+        quantize_h(0)
+        round_wy("scalar", 1, "wb_raw0")
+        quantize_wy(1)
+        round_wy("scalar", 2, "wy_bf0")
+        combine(1)
+        quantize_wy(2)
+        round_h("vector", 1, 0, HALF)
+        quantize_h(1)
+        for q in range(QUADS):
+            nc.sync.dma_start(out_3[0, 4 * q : 4 * q + 4, :].bitcast(I32), h_sc[32 * q : 32 * q + 4, :].bitcast(I32))
 
-        def direct(index, s, n, lo, hi):
-            cols = slice(P * n, P * (n + 1))
-            y_acc[index] = bank(index % 8, "y_acc%d" % index)
-            for a in range(PASSES):
-                scale = planes[:, a, WD_COL + P * n : WD_COL + P * (n + 1)]
-                times_v(y_acc[index], wd[:, a, cols].bitcast(FP8X4), scale, a, s, a == 0, False, lo, hi)
-
-        def detect(index, s, n, lo, hi):
+        pieces = [(n, s, 0, HALF) for s in range(HALVES) for n in range(N_TILES - s)]
+        pieces += [(N_TILES - 1, 1, 0, HALF // 2), (N_TILES - 1, 1, HALF // 2, HALF)]
+        y_banks = (4, 5, 6, 7, 4, 5, 0, 1, 2, 3, 6, 7, 4)
+        for index, (n, s, lo, hi) in enumerate(pieces):
             cols = slice(P * n, P * (n + 1))
             tokens = slice(HALF * s + lo, HALF * s + hi)
-            acc = y_acc[index]
+            y_acc = bank(y_banks[index], "y_acc%d" % index)
+            for a in range(PASSES):
+                scale = planes[a][:, WD_COL + P * n : WD_COL + P * (n + 1)]
+                times_v(y_acc, wd[:, a, cols].bitcast(FP8X4), scale, a, s, a == 0, False, lo, hi)
             nc.tensor.matmul_mx(
-                out=acc[:, 0 : hi - lo],
+                out=y_acc[:, 0 : hi - lo],
                 lhsT=wy_q[:, cols].bitcast(FP8X4),
                 lhsT_scale=wy_sc[:, cols],
                 rhs=h_q[:, tokens].bitcast(FP8X4),
@@ -236,32 +258,5 @@ def tile_list_branch_max_combining_kernel(
                 stop=True,
             )
             res = sb([P, hi - lo], F32, "y%d" % index)
-            nc.scalar.activation(res[:], acc[:, 0 : hi - lo], TANH, bias=bias[:, n : n + 1])
+            nc.scalar.activation(res[:], y_acc[:, 0 : hi - lo], TANH, bias=bias[:, n : n + 1])
             nc.sync.dma_start(out_0[cols, tokens], res[:])
-
-        multiply_a(0)
-        multiply_a(1)
-        combine(0)
-        wy_bf_all = sb([P, N * PACK], BF16, "wy_bf", "wb_raw0")
-        wy_bf = [wy_bf_all[:, WY_CHUNK * PACK * c : WY_CHUNK * PACK * (c + 1)] for c in range(N // WY_CHUNK)]
-        round_h(0)
-        quantize_h(0)
-        round_wy(0, "scalar")
-        quantize_wy(0)
-        round_wy(1, "scalar")
-        quantize_wy(1)
-        combine(1)
-        round_wy(2, "scalar")
-        quantize_wy(2)
-        round_h(1)
-        quantize_h(1)
-        for q in range(QUADS):
-            nc.gpsimd.dma_start(out_3[0, 4 * q : 4 * q + 4, :].bitcast(I32), h_sc[32 * q : 32 * q + 4, :].bitcast(I32))
-        pieces = [(s, n, 0, HALF) for s in range(HALVES) for n in range(N_TILES - s)]
-        pieces += [(1, N_TILES - 1, 0, HALF // 2), (1, N_TILES - 1, HALF // 2, HALF)]
-        for index in range(PACK):
-            direct(index, *pieces[index])
-        for index, piece in enumerate(pieces):
-            if index >= PACK:
-                direct(index, *piece)
-            detect(index, *piece)

@@ -26,6 +26,7 @@ HALVES = S // HALF
 N_TILES = N // P
 WY_CHUNK = 256
 QUADS = 4
+BY_PIECES = (0, 1, 2, N_TILES - 1)
 SCALAR_TOKENS = 160
 SC_ROWS = 32
 WB_COL, WD_COL, SC_COLS = S, S + H, S + H + N
@@ -151,10 +152,11 @@ def tile_list_branch_max_combining_kernel(
             times_v(acc, wa_q[:, a, cols].bitcast(FP8X4), wa_sc[:, a, cols], a, s, a == 0, a == PASSES - 1)
 
         b_acc = {(s, t): bank(PACK * s + t, "b_acc%d_%d" % (s, t)) for s in range(HALVES) for t in range(PACK)}
-        groups = [(s, t) for s in range(HALVES) for t in range(PACK)]
-        for a in range(PASSES):
-            for s, t in groups:
-                branch_b(b_acc[s, t], a, s, t)
+        groups = [(s, t) for t in range(PACK) for s in range(HALVES)]
+        for s, t in sorted(groups):
+            branch_b(b_acc[s, t], 0, s, t)
+        for s, t in groups:
+            branch_b(b_acc[s, t], 1, s, t)
 
         wa_q = sb([P, PASSES, H], U32, "wa_q")
         wa_sc = sb([P, PASSES, H], U8, "wa_sc")
@@ -171,25 +173,26 @@ def tile_list_branch_max_combining_kernel(
                 cols = slice(2 * P * u, 2 * P * (u + 1))
                 nc.vector.quantize_mx(out=wa_q[:, a, cols].bitcast(FP8X4), scales=wa_sc[:, a, cols], in_=wa_bf[a, u][:])
 
-        b_tiles = [sb([P, PACK, HALF], F32, "b_sb%d" % u, "wb_raw%d" % u) for u in range(2)]
         b_sb = {}
-        for index, (s, t) in enumerate(groups):
-            b_sb[s, t] = b_tiles[index // PACK][:, index % PACK, :]
-            nc.scalar.activation(b_sb[s, t], b_acc[s, t][:], COPY)
+        first = 0
+        for count, tag in ((4, "wb_raw0"), (2, "wb_raw1"), (1, "wa_bf1_0"), (1, "wa_bf1_1")):
+            tile = sb([P, count, HALF], F32, "b_sb%d" % first, tag)
+            for index, (s, t) in enumerate(groups[first : first + count]):
+                b_sb[s, t] = tile[:, index, :]
+                nc.scalar.activation(b_sb[s, t], b_acc[s, t][:], COPY)
+            first = first + count
 
         h = sb([P, PACK, S], F32, "h")
         h_out = out_1.rearrange("(p t) j -> p t j", t=PACK)
+        for s, t in groups:
+            a_acc = bank(PACK * s + t % 2, "a_acc%d_%d" % (s, t))
+            for a in range(PASSES):
+                branch_a(a_acc, a, s, t)
+            nc.vector.tensor_tensor(h[:, t, HALF * s : HALF * (s + 1)], a_acc[:], b_sb[s, t], MAX)
+            if s == HALVES - 1:
+                nc.sync.dma_start(h_out[:, t, :], h[:, t, :])
 
-        def combine(s):
-            tokens = slice(HALF * s, HALF * (s + 1))
-            for t in range(PACK):
-                a_acc = bank(t, "a_acc%d_%d" % (s, t))
-                for a in range(PASSES):
-                    branch_a(a_acc, a, s, t)
-                nc.vector.tensor_tensor(h[:, t, tokens], a_acc[:], b_sb[s, t], MAX)
-                nc.sync.dma_start(h_out[:, t, tokens], h[:, t, tokens])
-
-        wy_q = sb([P, N], U32, "wy_q")
+        wy_q = sb([P, N], U32, "wy_q", "wa_bf1_0")
         wy_sc = sb([P, N], U8, "wy_sc")
         wy_bf = {}
 
@@ -222,25 +225,25 @@ def tile_list_branch_max_combining_kernel(
             nc.vector.quantize_mx(out=h_q[:, tokens].bitcast(FP8X4), scales=h_sc[:, tokens], in_=h_bf[s][:])
             nc.sync.dma_start(words_out[:, tokens], h_q[:, tokens].bitcast(I32))
 
-        combine(0)
         round_wy("scalar", 0, "wy_bf0")
+        round_wy("scalar", 1, "wy_bf1")
         round_h("scalar", 0, 0, SCALAR_TOKENS)
+        round_wy("scalar", 2, "wa_bf1_1")
         round_h("vector", 0, SCALAR_TOKENS, HALF)
         quantize_wy(0)
         quantize_h(0)
-        round_wy("scalar", 1, "wb_raw0")
         quantize_wy(1)
-        round_wy("scalar", 2, "wy_bf0")
-        combine(1)
-        quantize_wy(2)
         round_h("vector", 1, 0, HALF)
+        quantize_wy(2)
         quantize_h(1)
         for q in range(QUADS):
             nc.sync.dma_start(out_3[0, 4 * q : 4 * q + 4, :].bitcast(I32), h_sc[32 * q : 32 * q + 4, :].bitcast(I32))
 
-        pieces = [(n, s, 0, HALF) for s in range(HALVES) for n in range(N_TILES - s)]
+        pieces = [(n, s, 0, HALF) for s in range(HALVES) for n in range(PACK)]
+        pieces += [(n, s, 0, HALF) for n in range(PACK, N_TILES) for s in range(HALVES)][:-1]
         pieces += [(N_TILES - 1, 1, 0, HALF // 2), (N_TILES - 1, 1, HALF // 2, HALF)]
-        y_banks = (4, 5, 6, 7, 4, 5, 0, 1, 2, 3, 6, 7, 4)
+        y_banks = (2, 6, 3, 7, 0, 4, 2, 6, 3, 7, 0, 4, 2)
+        res = [sb([P, S], F32, "y%d" % n) for n in range(N_TILES)]
         for index, (n, s, lo, hi) in enumerate(pieces):
             cols = slice(P * n, P * (n + 1))
             tokens = slice(HALF * s + lo, HALF * s + hi)
@@ -257,6 +260,8 @@ def tile_list_branch_max_combining_kernel(
                 start=False,
                 stop=True,
             )
-            res = sb([P, hi - lo], F32, "y%d" % index)
-            nc.scalar.activation(res[:], y_acc[:, 0 : hi - lo], TANH, bias=bias[:, n : n + 1])
-            nc.sync.dma_start(out_0[cols, tokens], res[:])
+            nc.scalar.activation(res[n][:, tokens], y_acc[:, 0 : hi - lo], TANH, bias=bias[:, n : n + 1])
+            if n in BY_PIECES:
+                nc.sync.dma_start(out_0[cols, tokens], res[n][:, tokens])
+            elif s == HALVES - 1:
+                nc.sync.dma_start(out_0[cols, :], res[n][:])

@@ -26,10 +26,16 @@ HALVES = S // HALF
 N_TILES = N // P
 WY_CHUNK = 256
 QUADS = 4
+BANKS = 8
+AHEAD = 5
 BY_PIECES = (0, 1, 2, N_TILES - 1)
 SCALAR_TOKENS = 160
 SC_ROWS = 32
-WB_COL, WD_COL, SC_COLS = S, S + H, S + H + N
+WD_ROW = 4
+H_ROW = 8
+WA_BYTES = PACK * H * 4
+WY_BYTES = PACK * N * 4
+TAB_AT = (PASSES * WA_BYTES, PASSES * WA_BYTES + 2 * H + WY_BYTES)
 
 
 def tile_list_branch_max_combining_kernel(
@@ -38,6 +44,7 @@ def tile_list_branch_max_combining_kernel(
     nc = tc.nc
     with ExitStack() as ctx:
         keep = ctx.enter_context(tc.tile_pool(name="keep", bufs=1))
+        placed = ctx.enter_context(tc.tile_pool(name="placed", bufs=1))
         psum = ctx.enter_context(tc.psum_pool(name="psum", bufs=1))
 
         def sb(shape, dtype, name, tag=None):
@@ -54,32 +61,19 @@ def tile_list_branch_max_combining_kernel(
 
         offsets = keep.tile([P, S // 16], U16, name="offsets")
         tab_sc = sb([P, T], U8, "tab_sc")
-        wb_sc_raw = sb([P, H], U8, "wb_sc_raw")
-        planes = [sb([P, SC_COLS], U8, "plane%d" % a) for a in range(PASSES)]
+        wb_sc_raw = placed.tile([P, H], U8, name="wb_sc_raw", offset=WA_BYTES - H // 2)
+        planes = [sb([P, S + H], U8, "plane0")]
         for lo, hi in ((SC_ROWS, 64), (64, P)):
             nc.vector.memset(tab_sc[lo:hi, :].bitcast(I32), 0)
             nc.vector.memset(wb_sc_raw[lo:hi, :].bitcast(I32), 0)
-            nc.vector.memset(planes[0][lo:hi, WD_COL:SC_COLS].bitcast(I32), 0)
-
         by_rows = sb([P, P], F32, "by_rows")
         nc.gpsimd.memset(by_rows[:], 0.0)
         identity = sb([P, P], F32, "identity")
         make_identity(nc, identity[:])
-        nc.gpsimd.memset(planes[1][:].bitcast(I32), 0)
-        nc.scalar.dma_start(by_rows[0:N_TILES, :], by.rearrange("(c p) -> c p", p=P))
-        by_cols = psum.tile([P, P], F32, name="by_cols", tag="bank7")
-        nc.tensor.transpose(by_cols[:], by_rows[:], identity[:])
-        bias = sb([P, N_TILES], F32, "bias")
-        nc.scalar.activation(bias[:], by_cols[:, 0:N_TILES], COPY)
 
-        def load_tab(a, tag):
-            tile = sb([P, T], I32, "tab%d" % a, tag)
+        def load_tab(a):
+            tile = placed.tile([P, T], I32, name="tab%d" % a, offset=TAB_AT[a])
             nc.sync.dma_start(tile[:], tab_words[a].rearrange("p t i -> p (t i)").bitcast(I32))
-            return tile
-
-        def load_wa(a, tag):
-            tile = sb([P, PACK, H], F32, "wa_raw%d" % a, tag)
-            nc.sync.dma_start(tile[:], wa[512 * a : 512 * (a + 1), :].rearrange("(p j) c -> p j c", j=PACK))
             return tile
 
         def load_scale_rows(tile, scales):
@@ -88,43 +82,67 @@ def tile_list_branch_max_combining_kernel(
         nc.sync.dma_start(offsets[:], offs)
         load_scale_rows(tab_sc[:], tab_scales)
         load_scale_rows(wb_sc_raw[:], wb_scales)
-        load_scale_rows(planes[0][:, WD_COL:SC_COLS], wd_scales)
-        wb_raw = [sb([P, 2 * H], U8, "wb_raw%d" % a) for a in range(PASSES)]
-        for a in range(PASSES):
-            nc.sync.dma_start(wb_raw[a][:].bitcast(I32), wb_words[a].bitcast(I32))
-        tab = [load_tab(a, "tab%d" % a) for a in range(PASSES)]
+        wb_raw = sb([P, PASSES, H // 2], I32, "wb_raw")
+        nc.sync.dma_start(wb_raw[:], wb_words.bitcast(I32).rearrange("a p c -> p a c"))
+        tab = [load_tab(0)]
+        nc.sync.dma_start(by_rows[0:N_TILES, :], by.rearrange("(c p) -> c p", p=P))
+        tab.append(load_tab(1))
 
-        nc.vector.tensor_copy(
-            planes[0][:, WB_COL:WD_COL].rearrange("p (t m) -> p t m", t=PACK),
-            wb_sc_raw[:].rearrange("p (m t) -> p t m", t=PACK),
-        )
+        by_cols = psum.tile([P, P], F32, name="by_cols", tag="bank%d" % (BANKS - 1))
+        nc.tensor.transpose(by_cols[:], by_rows[:], identity[:])
+        bias = sb([P, N_TILES], F32, "bias")
+        nc.scalar.activation(bias[:], by_cols[:, 0:N_TILES], COPY)
+
         v_sc = sb([P, S], U8, "v_sc")
         nc.vector.tensor_copy(v_sc[:], tab_sc[:].indirect(offsets[:]))
         nc.vector.tensor_copy(planes[0][:, 0:S].bitcast(I32), v_sc[:].bitcast(I32))
+        nc.vector.tensor_copy(
+            planes[0][:, S : S + H].rearrange("p (t m) -> p t m", t=PACK),
+            wb_sc_raw[:].rearrange("p (m t) -> p t m", t=PACK),
+        )
+        planes.append(sb([P, S + H], U8, "plane1", "v_sc"))
+        nc.vector.memset(planes[1][:].bitcast(I32), 0)
+        wa_raw = []
+
+        def load_wa(a):
+            wa_raw.append(placed.tile([P, PACK, H], F32, name="wa_raw%d" % a, offset=WA_BYTES * a))
+            nc.sync.dma_start(wa_raw[a][:], wa[512 * a : 512 * (a + 1), :].rearrange("(p j) c -> p j c", j=PACK))
+
         for a in range(PASSES):
             for q in range(QUADS):
                 row = 16 * a + 4 * q
                 if row > 0:
-                    nc.scalar.dma_start(planes[a][32 * q : 32 * q + 4, :].bitcast(I32), planes[0][row : row + 4, :].bitcast(I32))
+                    nc.sync.dma_start(planes[a][32 * q : 32 * q + 4, :].bitcast(I32), planes[0][row : row + 4, :].bitcast(I32))
+            if a == 0:
+                load_wa(0)
 
-        wb = sb([P, PASSES, 2 * H], U8, "wb", "v_sc")
-        wa_raw = []
-        for a in range(PASSES):
-            nc.vector.tensor_copy(
-                wb[:, a, :].bitcast(U16).rearrange("p (t m) -> p t m", t=PACK),
-                wb_raw[a][:].bitcast(U16).rearrange("p (m t) -> p t m", t=PACK),
-            )
-            wa_raw.append(load_wa(a, "wb_raw%d" % a))
-
+        load_wa(1)
+        wb = []
         v = {}
         for a in range(PASSES):
+            if a == 0:
+                wb.append(sb([P, 2 * H], U8, "wb0"))
+            else:
+                wb.append(placed.tile([P, 2 * H], U8, name="wb1", offset=TAB_AT[0], align_bytes=64))
+            nc.vector.tensor_copy(
+                wb[a][:].bitcast(U16).rearrange("p (t m) -> p t m", t=PACK),
+                wb_raw[:, a, :].bitcast(U16).rearrange("p (m t) -> p t m", t=PACK),
+            )
             for s in range(HALVES):
                 v[a, s] = sb([P, HALF], U32, "v%d_%d" % (a, s))
                 cols = HALF // 16
                 nc.vector.tensor_copy(v[a, s][:], tab[a][:].bitcast(U32).indirect(offsets[:, cols * s : cols * (s + 1)]))
-        wy_raw = sb([P, PACK, N], F32, "wy_raw", "tab0")
+
+        wd_sc = wb_raw[:].rearrange("p a c -> p (a c)")[:, 0 : PASSES * N // 4].bitcast(U8)
+        wd_rows = wd_scales.bitcast(I32).rearrange("a q c -> q a c")
+        for q in range(QUADS):
+            nc.sync.dma_start(
+                wd_sc[32 * q + WD_ROW : 32 * q + WD_ROW + 4, :].bitcast(I32).rearrange("p (a c) -> p a c", a=PASSES),
+                wd_rows[4 * q : 4 * q + 4],
+            )
+        wy_raw = placed.tile([P, PACK, N], F32, name="wy_raw", offset=TAB_AT[0] + 2 * H)
         nc.sync.dma_start(wy_raw[:], wy.rearrange("(p j) n -> p j n", j=PACK))
-        wd = sb([P, PASSES, N], I32, "wd", "tab1")
+        wd = placed.tile([P, PASSES, N], I32, name="wd", offset=TAB_AT[1], align_bytes=64)
         for a in range(PASSES):
             nc.sync.dma_start(wd[:, a, :], wd_words[a].rearrange("p c i -> p (c i)").bitcast(I32))
 
@@ -142,8 +160,8 @@ def tile_list_branch_max_combining_kernel(
         def branch_b(acc, a, s, t):
             times_v(
                 acc,
-                wb[:, a, 2 * P * t : 2 * P * (t + 1)].bitcast(FP4X4),
-                planes[a][:, WB_COL + P * t : WB_COL + P * (t + 1)],
+                wb[a][:, 2 * P * t : 2 * P * (t + 1)].bitcast(FP4X4),
+                planes[a][:, S + P * t : S + P * (t + 1)],
                 a, s, a == 0, a == PASSES - 1,
             )
 
@@ -175,8 +193,11 @@ def tile_list_branch_max_combining_kernel(
 
         b_sb = {}
         first = 0
-        for count, tag in ((4, "wb_raw0"), (2, "wb_raw1"), (1, "wa_bf1_0"), (1, "wa_bf1_1")):
-            tile = sb([P, count, HALF], F32, "b_sb%d" % first, tag)
+        for count, tag in ((4, 0), (2, 1), (1, "wa_bf1_0"), (1, "wa_bf1_1")):
+            if count > 1:
+                tile = placed.tile([P, count, HALF], F32, name="b_sb%d" % first, offset=WA_BYTES * tag)
+            else:
+                tile = sb([P, count, HALF], F32, "b_sb%d" % first, tag)
             for index, (s, t) in enumerate(groups[first : first + count]):
                 b_sb[s, t] = tile[:, index, :]
                 nc.scalar.activation(b_sb[s, t], b_acc[s, t][:], COPY)
@@ -192,7 +213,7 @@ def tile_list_branch_max_combining_kernel(
             if s == HALVES - 1:
                 nc.sync.dma_start(h_out[:, t, :], h[:, t, :])
 
-        wy_q = sb([P, N], U32, "wy_q", "wa_bf1_0")
+        wy_q = {}
         wy_sc = sb([P, N], U8, "wy_sc")
         wy_bf = {}
 
@@ -204,11 +225,12 @@ def tile_list_branch_max_combining_kernel(
                 wy_raw[:, :, WY_CHUNK * c : WY_CHUNK * (c + 1)].rearrange("p j (c i) -> p c j i", i=4),
             )
 
-        def quantize_wy(c):
+        def quantize_wy(c, codes):
+            wy_q[c] = codes
             cols = slice(WY_CHUNK * c, WY_CHUNK * (c + 1))
-            nc.vector.quantize_mx(out=wy_q[:, cols].bitcast(FP8X4), scales=wy_sc[:, cols], in_=wy_bf[c])
+            nc.vector.quantize_mx(out=codes.bitcast(FP8X4), scales=wy_sc[:, cols], in_=wy_bf[c])
 
-        h_bf = [sb([P, HALF * PACK], BF16, "h_bf%d" % s, "h_bf") for s in range(HALVES)]
+        h_bf = {}
         h_q = sb([P, S], U32, "h_q")
         h_sc = sb([P, S], U8, "h_sc")
         words_out = out_2[0].rearrange("p m t -> p (m t)").bitcast(I32)
@@ -222,46 +244,66 @@ def tile_list_branch_max_combining_kernel(
 
         def quantize_h(s):
             tokens = slice(HALF * s, HALF * (s + 1))
-            nc.vector.quantize_mx(out=h_q[:, tokens].bitcast(FP8X4), scales=h_sc[:, tokens], in_=h_bf[s][:])
+            nc.vector.quantize_mx(out=h_q[:, tokens].bitcast(FP8X4), scales=h_sc[H_ROW:P, tokens], in_=h_bf[s][:])
             nc.sync.dma_start(words_out[:, tokens], h_q[:, tokens].bitcast(I32))
 
-        round_wy("scalar", 0, "wy_bf0")
-        round_wy("scalar", 1, "wy_bf1")
+        for c in range(N // WY_CHUNK):
+            round_wy("scalar", c, "wy_bf%d" % c)
+        quantize_wy(0, sb([P, WY_CHUNK], U32, "wy_q0")[:])
+        h_bf[0] = sb([P, HALF * PACK], BF16, "h_bf0", "wy_bf0")
         round_h("scalar", 0, 0, SCALAR_TOKENS)
-        round_wy("scalar", 2, "wa_bf1_1")
         round_h("vector", 0, SCALAR_TOKENS, HALF)
-        quantize_wy(0)
         quantize_h(0)
-        quantize_wy(1)
+        wy_rest = sb([P, 2, WY_CHUNK], U32, "wy_rest", "wy_bf0")
+        quantize_wy(1, wy_rest[:, 0, :])
+        h_bf[1] = sb([P, HALF * PACK], BF16, "h_bf1", "wy_bf1")
         round_h("vector", 1, 0, HALF)
-        quantize_wy(2)
+        quantize_wy(2, wy_rest[:, 1, :])
         quantize_h(1)
         for q in range(QUADS):
-            nc.sync.dma_start(out_3[0, 4 * q : 4 * q + 4, :].bitcast(I32), h_sc[32 * q : 32 * q + 4, :].bitcast(I32))
+            nc.sync.dma_start(out_3[0, 4 * q : 4 * q + 4, :].bitcast(I32), h_sc[32 * q + H_ROW : 32 * q + H_ROW + 4, :].bitcast(I32))
 
         pieces = [(n, s, 0, HALF) for s in range(HALVES) for n in range(PACK)]
         pieces += [(n, s, 0, HALF) for n in range(PACK, N_TILES) for s in range(HALVES)][:-1]
         pieces += [(N_TILES - 1, 1, 0, HALF // 2), (N_TILES - 1, 1, HALF // 2, HALF)]
         y_banks = (2, 6, 3, 7, 0, 4, 2, 6, 3, 7, 0, 4, 2)
         res = [sb([P, S], F32, "y%d" % n) for n in range(N_TILES)]
-        for index, (n, s, lo, hi) in enumerate(pieces):
+        y_acc = {}
+
+        def direct(index):
+            n, s, lo, hi = pieces[index]
+            y_acc[index] = bank(y_banks[index], "y_acc%d" % index)
+            for a in range(PASSES):
+                scale = wd_sc[WD_ROW:P, N * a + P * n : N * a + P * (n + 1)]
+                times_v(y_acc[index], wd[:, a, P * n : P * (n + 1)].bitcast(FP8X4), scale, a, s, a == 0, False, lo, hi)
+
+        def close(index):
+            n, s, lo, hi = pieces[index]
             cols = slice(P * n, P * (n + 1))
             tokens = slice(HALF * s + lo, HALF * s + hi)
-            y_acc = bank(y_banks[index], "y_acc%d" % index)
-            for a in range(PASSES):
-                scale = planes[a][:, WD_COL + P * n : WD_COL + P * (n + 1)]
-                times_v(y_acc, wd[:, a, cols].bitcast(FP8X4), scale, a, s, a == 0, False, lo, hi)
             nc.tensor.matmul_mx(
-                out=y_acc[:, 0 : hi - lo],
-                lhsT=wy_q[:, cols].bitcast(FP8X4),
+                out=y_acc[index][:, 0 : hi - lo],
+                lhsT=wy_q[n // 2][:, P * (n % 2) : P * (n % 2 + 1)].bitcast(FP8X4),
                 lhsT_scale=wy_sc[:, cols],
                 rhs=h_q[:, tokens].bitcast(FP8X4),
-                rhs_scale=h_sc[:, tokens],
+                rhs_scale=h_sc[H_ROW:P, tokens],
                 start=False,
                 stop=True,
             )
-            nc.scalar.activation(res[n][:, tokens], y_acc[:, 0 : hi - lo], TANH, bias=bias[:, n : n + 1])
+            nc.scalar.activation(res[n][:, tokens], y_acc[index][:, 0 : hi - lo], TANH, bias=bias[:, n : n + 1])
             if n in BY_PIECES:
                 nc.sync.dma_start(out_0[cols, tokens], res[n][:, tokens])
             elif s == HALVES - 1:
                 nc.sync.dma_start(out_0[cols, :], res[n][:])
+
+        for index in range(AHEAD):
+            direct(index)
+        for index in range(PACK):
+            close(index)
+        for index in range(AHEAD, 2 * PACK):
+            direct(index)
+        for index in range(PACK, 2 * PACK):
+            close(index)
+        for index in range(2 * PACK, len(pieces)):
+            direct(index)
+            close(index)

@@ -27,9 +27,9 @@ N_TILES = N // P
 WY_CHUNK = 256
 QUADS = 4
 BANKS = 8
-AHEAD = 5
-BY_PIECES = (0, 1, 2, N_TILES - 1)
-SCALAR_TOKENS = 160
+H_PITCH = S + HALF
+WARM_UPS = 4
+AHEAD = 6
 SC_ROWS = 32
 WD_ROW = 4
 H_ROW = 8
@@ -146,6 +146,18 @@ def tile_list_branch_max_combining_kernel(
         for a in range(PASSES):
             nc.sync.dma_start(wd[:, a, :], wd_words[a].rearrange("p c i -> p (c i)").bitcast(I32))
 
+        warm = bank(BANKS - 2, "warm")
+        for index in range(WARM_UPS):
+            nc.tensor.matmul_mx(
+                out=warm[:],
+                lhsT=tab[0][:, 0:P].bitcast(FP8X4),
+                lhsT_scale=tab_sc[:, 0:P],
+                rhs=tab[0][:, 0:HALF].bitcast(FP8X4),
+                rhs_scale=tab_sc[:, 0:HALF],
+                start=True,
+                stop=True,
+            )
+
         def times_v(acc, lhsT, lhsT_scale, a, s, start, stop, lo=0, hi=HALF):
             nc.tensor.matmul_mx(
                 out=acc[:, 0 : hi - lo],
@@ -192,18 +204,12 @@ def tile_list_branch_max_combining_kernel(
                 nc.vector.quantize_mx(out=wa_q[:, a, cols].bitcast(FP8X4), scales=wa_sc[:, a, cols], in_=wa_bf[a, u][:])
 
         b_sb = {}
-        first = 0
-        for count, tag in ((4, 0), (2, 1), (1, "wa_bf1_0"), (1, "wa_bf1_1")):
-            if count > 1:
-                tile = placed.tile([P, count, HALF], F32, name="b_sb%d" % first, offset=WA_BYTES * tag)
-            else:
-                tile = sb([P, count, HALF], F32, "b_sb%d" % first, tag)
-            for index, (s, t) in enumerate(groups[first : first + count]):
-                b_sb[s, t] = tile[:, index, :]
-                nc.scalar.activation(b_sb[s, t], b_acc[s, t][:], COPY)
-            first = first + count
+        for s, t in groups:
+            b_sb[s, t] = sb([P, HALF], F32, "b_sb%d_%d" % (s, t))[:]
+            nc.scalar.activation(b_sb[s, t], b_acc[s, t][:], COPY)
 
-        h = sb([P, PACK, S], F32, "h")
+        h_rows = sb([P, PACK * H_PITCH], F32, "h")
+        h = h_rows[:].rearrange("p (t j) -> p t j", t=PACK)
         h_out = out_1.rearrange("(p t) j -> p t j", t=PACK)
         for s, t in groups:
             a_acc = bank(PACK * s + t % 2, "a_acc%d_%d" % (s, t))
@@ -211,35 +217,34 @@ def tile_list_branch_max_combining_kernel(
                 branch_a(a_acc, a, s, t)
             nc.vector.tensor_tensor(h[:, t, HALF * s : HALF * (s + 1)], a_acc[:], b_sb[s, t], MAX)
             if s == HALVES - 1:
-                nc.sync.dma_start(h_out[:, t, :], h[:, t, :])
+                nc.sync.dma_start(h_out[:, t, :], h[:, t, 0:S])
 
-        wy_q = {}
+        wy_q = sb([P, N], U32, "wy_q")
         wy_sc = sb([P, N], U8, "wy_sc")
-        wy_bf = {}
+        wy_bf = [h_rows[:, S:H_PITCH].bitcast(BF16)]
+        wy_bf += [sb([P, WY_CHUNK * PACK], BF16, "wy_bf%d" % c)[:] for c in (1, 2)]
 
-        def round_wy(engine, c, tag):
-            wy_bf[c] = sb([P, WY_CHUNK * PACK], BF16, "wy_bf%d" % c, tag)[:]
-            cast(
-                engine,
+        def round_wy(c):
+            nc.scalar.activation(
                 wy_bf[c].rearrange("p (c i j) -> p c j i", i=4, j=PACK),
                 wy_raw[:, :, WY_CHUNK * c : WY_CHUNK * (c + 1)].rearrange("p j (c i) -> p c j i", i=4),
+                COPY,
             )
 
-        def quantize_wy(c, codes):
-            wy_q[c] = codes
+        def quantize_wy(c):
             cols = slice(WY_CHUNK * c, WY_CHUNK * (c + 1))
-            nc.vector.quantize_mx(out=codes.bitcast(FP8X4), scales=wy_sc[:, cols], in_=wy_bf[c])
+            nc.vector.quantize_mx(out=wy_q[:, cols].bitcast(FP8X4), scales=wy_sc[:, cols], in_=wy_bf[c])
 
-        h_bf = {}
+        h_bf = [sb([P, HALF * PACK], BF16, "h_bf%d" % s) for s in range(HALVES)]
         h_q = sb([P, S], U32, "h_q")
         h_sc = sb([P, S], U8, "h_sc")
         words_out = out_2[0].rearrange("p m t -> p (m t)").bitcast(I32)
 
-        def round_h(engine, s, lo, hi):
+        def round_h(engine, s):
             cast(
                 engine,
-                h_bf[s][:, PACK * lo : PACK * hi].rearrange("p (c i t) -> p c t i", i=4, t=PACK),
-                h[:, :, HALF * s + lo : HALF * s + hi].rearrange("p t (c i) -> p c t i", i=4),
+                h_bf[s][:].rearrange("p (c i t) -> p c t i", i=4, t=PACK),
+                h[:, :, HALF * s : HALF * (s + 1)].rearrange("p t (c i) -> p c t i", i=4),
             )
 
         def quantize_h(s):
@@ -247,26 +252,21 @@ def tile_list_branch_max_combining_kernel(
             nc.vector.quantize_mx(out=h_q[:, tokens].bitcast(FP8X4), scales=h_sc[H_ROW:P, tokens], in_=h_bf[s][:])
             nc.sync.dma_start(words_out[:, tokens], h_q[:, tokens].bitcast(I32))
 
-        for c in range(N // WY_CHUNK):
-            round_wy("scalar", c, "wy_bf%d" % c)
-        quantize_wy(0, sb([P, WY_CHUNK], U32, "wy_q0")[:])
-        h_bf[0] = sb([P, HALF * PACK], BF16, "h_bf0", "wy_bf0")
-        round_h("scalar", 0, 0, SCALAR_TOKENS)
-        round_h("vector", 0, SCALAR_TOKENS, HALF)
-        quantize_h(0)
-        wy_rest = sb([P, 2, WY_CHUNK], U32, "wy_rest", "wy_bf0")
-        quantize_wy(1, wy_rest[:, 0, :])
-        h_bf[1] = sb([P, HALF * PACK], BF16, "h_bf1", "wy_bf1")
-        round_h("vector", 1, 0, HALF)
-        quantize_wy(2, wy_rest[:, 1, :])
+        round_wy(0)
+        round_wy(1)
+        quantize_wy(0)
+        round_h("scalar", 0)
+        round_wy(2)
+        round_h("vector", 1)
         quantize_h(1)
+        quantize_h(0)
+        quantize_wy(1)
+        quantize_wy(2)
         for q in range(QUADS):
             nc.sync.dma_start(out_3[0, 4 * q : 4 * q + 4, :].bitcast(I32), h_sc[32 * q + H_ROW : 32 * q + H_ROW + 4, :].bitcast(I32))
 
-        pieces = [(n, s, 0, HALF) for s in range(HALVES) for n in range(PACK)]
-        pieces += [(n, s, 0, HALF) for n in range(PACK, N_TILES) for s in range(HALVES)][:-1]
-        pieces += [(N_TILES - 1, 1, 0, HALF // 2), (N_TILES - 1, 1, HALF // 2, HALF)]
-        y_banks = (2, 6, 3, 7, 0, 4, 2, 6, 3, 7, 0, 4, 2)
+        pieces = [(n, s, 0, HALF) for n in range(N_TILES) for s in (1, 0)]
+        y_banks = (2, 6, 3, 7, 0, 4) * 2
         res = [sb([P, S], F32, "y%d" % n) for n in range(N_TILES)]
         y_acc = {}
 
@@ -283,7 +283,7 @@ def tile_list_branch_max_combining_kernel(
             tokens = slice(HALF * s + lo, HALF * s + hi)
             nc.tensor.matmul_mx(
                 out=y_acc[index][:, 0 : hi - lo],
-                lhsT=wy_q[n // 2][:, P * (n % 2) : P * (n % 2 + 1)].bitcast(FP8X4),
+                lhsT=wy_q[:, cols].bitcast(FP8X4),
                 lhsT_scale=wy_sc[:, cols],
                 rhs=h_q[:, tokens].bitcast(FP8X4),
                 rhs_scale=h_sc[H_ROW:P, tokens],
@@ -291,19 +291,12 @@ def tile_list_branch_max_combining_kernel(
                 stop=True,
             )
             nc.scalar.activation(res[n][:, tokens], y_acc[index][:, 0 : hi - lo], TANH, bias=bias[:, n : n + 1])
-            if n in BY_PIECES:
-                nc.sync.dma_start(out_0[cols, tokens], res[n][:, tokens])
-            elif s == HALVES - 1:
+            if s == 0:
                 nc.sync.dma_start(out_0[cols, :], res[n][:])
 
         for index in range(AHEAD):
             direct(index)
-        for index in range(PACK):
-            close(index)
-        for index in range(AHEAD, 2 * PACK):
-            direct(index)
-        for index in range(PACK, 2 * PACK):
-            close(index)
-        for index in range(2 * PACK, len(pieces)):
-            direct(index)
+        for index in range(len(pieces)):
+            if index >= AHEAD:
+                direct(index)
             close(index)

@@ -27,9 +27,9 @@ N_TILES = N // P
 WY_CHUNK = 256
 QUADS = 4
 BANKS = 8
-H_PITCH = S + HALF
+QUARTER = HALF // 2
 WARM_UPS = 4
-AHEAD = 6
+AHEAD = 14
 SC_ROWS = 32
 WD_ROW = 4
 H_ROW = 8
@@ -140,7 +140,7 @@ def tile_list_branch_max_combining_kernel(
                 wd_sc[32 * q + WD_ROW : 32 * q + WD_ROW + 4, :].bitcast(I32).rearrange("p (a c) -> p a c", a=PASSES),
                 wd_rows[4 * q : 4 * q + 4],
             )
-        wy_raw = placed.tile([P, PACK, N], F32, name="wy_raw", offset=TAB_AT[0] + 2 * H)
+        wy_raw = placed.tile([P, PACK, N], F32, name="wy_raw", offset=TAB_AT[0] + 2 * H, align_bytes=64)
         nc.sync.dma_start(wy_raw[:], wy.rearrange("(p j) n -> p j n", j=PACK))
         wd = placed.tile([P, PASSES, N], I32, name="wd", offset=TAB_AT[1], align_bytes=64)
         for a in range(PASSES):
@@ -178,104 +178,115 @@ def tile_list_branch_max_combining_kernel(
             )
 
         def branch_a(acc, a, s, t):
-            cols = slice(P * t, P * (t + 1))
-            times_v(acc, wa_q[:, a, cols].bitcast(FP8X4), wa_sc[:, a, cols], a, s, a == 0, a == PASSES - 1)
+            codes = wa_q[a, t // 2][:, P * (t % 2) : P * (t % 2 + 1)].bitcast(FP8X4)
+            times_v(acc, codes, wa_sc[:, a, P * t : P * (t + 1)], a, s, a == 0, a == PASSES - 1)
 
         b_acc = {(s, t): bank(PACK * s + t, "b_acc%d_%d" % (s, t)) for s in range(HALVES) for t in range(PACK)}
-        groups = [(s, t) for t in range(PACK) for s in range(HALVES)]
-        for s, t in sorted(groups):
-            branch_b(b_acc[s, t], 0, s, t)
-        for s, t in groups:
-            branch_b(b_acc[s, t], 1, s, t)
+        groups = [(s, t) for t in range(2) for s in range(HALVES)]
+        groups += [(s, t) for s in range(HALVES) for t in range(2, PACK)]
+        for a in range(PASSES):
+            for s, t in sorted(groups):
+                branch_b(b_acc[s, t], a, s, t)
 
-        wa_q = sb([P, PASSES, H], U32, "wa_q")
+        wa_q = {}
         wa_sc = sb([P, PASSES, H], U8, "wa_sc")
         wa_bf = {}
-        for a in range(PASSES):
-            for u in range(2):
-                wa_bf[a, u] = sb([P, 2 * P * PACK], BF16, "wa_bf%d_%d" % (a, u))
-                cast(
-                    "scalar" if (a, u) == (0, 0) else "vector",
-                    wa_bf[a, u][:].rearrange("p (t m j) -> p m j t", t=2, j=PACK),
-                    wa_raw[a][:].rearrange("p j (m t) -> p m j t", t=PACK)[:, :, :, 2 * u : 2 * u + 2],
-                )
-            for u in range(2):
-                cols = slice(2 * P * u, 2 * P * (u + 1))
-                nc.vector.quantize_mx(out=wa_q[:, a, cols].bitcast(FP8X4), scales=wa_sc[:, a, cols], in_=wa_bf[a, u][:])
+
+        def round_wa(engine, a, u):
+            wa_bf[a, u] = sb([P, 2 * P * PACK], BF16, "wa_bf%d_%d" % (a, u))
+            cast(
+                engine,
+                wa_bf[a, u][:].rearrange("p (t m j) -> p m j t", t=2, j=PACK),
+                wa_raw[a][:].rearrange("p j (m t) -> p m j t", t=PACK)[:, :, :, 2 * u : 2 * u + 2],
+            )
+
+        def quantize_wa(a, u, tag=None):
+            wa_q[a, u] = sb([P, 2 * P], U32, "wa_q%d_%d" % (a, u), tag)
+            cols = slice(2 * P * u, 2 * P * (u + 1))
+            nc.vector.quantize_mx(out=wa_q[a, u][:].bitcast(FP8X4), scales=wa_sc[:, a, cols], in_=wa_bf[a, u][:])
+
+        round_wa("scalar", 0, 0)
+        round_wa("vector", 0, 1)
+        quantize_wa(0, 0)
+        round_wa("vector", 1, 0)
+        round_wa("vector", 1, 1)
+        quantize_wa(1, 0)
+        quantize_wa(0, 1, "wa_bf1_0")
+        quantize_wa(1, 1)
 
         b_sb = {}
         for s, t in groups:
             b_sb[s, t] = sb([P, HALF], F32, "b_sb%d_%d" % (s, t))[:]
             nc.scalar.activation(b_sb[s, t], b_acc[s, t][:], COPY)
 
-        h_rows = sb([P, PACK * H_PITCH], F32, "h")
-        h = h_rows[:].rearrange("p (t j) -> p t j", t=PACK)
+        h = sb([P, PACK, S], F32, "h")
         h_out = out_1.rearrange("(p t) j -> p t j", t=PACK)
         for s, t in groups:
-            a_acc = bank(PACK * s + t % 2, "a_acc%d_%d" % (s, t))
+            a_acc = bank(PACK * s + t, "a_acc%d_%d" % (s, t))
             for a in range(PASSES):
                 branch_a(a_acc, a, s, t)
             nc.vector.tensor_tensor(h[:, t, HALF * s : HALF * (s + 1)], a_acc[:], b_sb[s, t], MAX)
             if s == HALVES - 1:
-                nc.sync.dma_start(h_out[:, t, :], h[:, t, 0:S])
+                nc.sync.dma_start(h_out[:, t, :], h[:, t, :])
 
         wy_q = sb([P, N], U32, "wy_q")
         wy_sc = sb([P, N], U8, "wy_sc")
-        wy_bf = [h_rows[:, S:H_PITCH].bitcast(BF16)]
-        wy_bf += [sb([P, WY_CHUNK * PACK], BF16, "wy_bf%d" % c)[:] for c in (1, 2)]
+        wy_bf = [sb([P, WY_CHUNK * PACK], BF16, "wy_bf%d" % c)[:] for c in range(N // WY_CHUNK)]
 
-        def round_wy(c):
-            nc.scalar.activation(
+        def round_wy(engine, c):
+            cast(
+                engine,
                 wy_bf[c].rearrange("p (c i j) -> p c j i", i=4, j=PACK),
                 wy_raw[:, :, WY_CHUNK * c : WY_CHUNK * (c + 1)].rearrange("p j (c i) -> p c j i", i=4),
-                COPY,
             )
 
         def quantize_wy(c):
             cols = slice(WY_CHUNK * c, WY_CHUNK * (c + 1))
             nc.vector.quantize_mx(out=wy_q[:, cols].bitcast(FP8X4), scales=wy_sc[:, cols], in_=wy_bf[c])
 
-        h_bf = [sb([P, HALF * PACK], BF16, "h_bf%d" % s) for s in range(HALVES)]
         h_q = sb([P, S], U32, "h_q")
         h_sc = sb([P, S], U8, "h_sc")
         words_out = out_2[0].rearrange("p m t -> p (m t)").bitcast(I32)
 
-        def round_h(engine, s):
+        def round_h(engine, rounded, lo, hi):
             cast(
                 engine,
-                h_bf[s][:].rearrange("p (c i t) -> p c t i", i=4, t=PACK),
-                h[:, :, HALF * s : HALF * (s + 1)].rearrange("p t (c i) -> p c t i", i=4),
+                rounded.rearrange("p (c i t) -> p c t i", i=4, t=PACK),
+                h[:, :, lo:hi].rearrange("p t (c i) -> p c t i", i=4),
             )
 
-        def quantize_h(s):
-            tokens = slice(HALF * s, HALF * (s + 1))
-            nc.vector.quantize_mx(out=h_q[:, tokens].bitcast(FP8X4), scales=h_sc[H_ROW:P, tokens], in_=h_bf[s][:])
-            nc.sync.dma_start(words_out[:, tokens], h_q[:, tokens].bitcast(I32))
+        def quantize_h(rounded, lo, hi):
+            nc.vector.quantize_mx(out=h_q[:, lo:hi].bitcast(FP8X4), scales=h_sc[H_ROW:P, lo:hi], in_=rounded)
 
-        round_wy(0)
-        round_wy(1)
+        round_wy("scalar", 0)
+        round_wy("scalar", 1)
         quantize_wy(0)
-        round_h("scalar", 0)
-        round_wy(2)
-        round_h("vector", 1)
-        quantize_h(1)
-        quantize_h(0)
+        quarters = [wy_raw[:, j, 0 : 2 * WY_CHUNK].bitcast(BF16) for j in range(2)]
+        for j in range(2):
+            round_h("scalar", quarters[j], QUARTER * j, QUARTER * (j + 1))
+        second = sb([P, HALF * PACK], BF16, "h_bf1", "wy_bf0")
+        round_h("vector", second[:], HALF, S)
+        quantize_h(second[:], HALF, S)
+        for j in range(2):
+            quantize_h(quarters[j], QUARTER * j, QUARTER * (j + 1))
+        nc.sync.dma_start(words_out, h_q[:].bitcast(I32))
         quantize_wy(1)
+        round_wy("vector", 2)
         quantize_wy(2)
         for q in range(QUADS):
             nc.sync.dma_start(out_3[0, 4 * q : 4 * q + 4, :].bitcast(I32), h_sc[32 * q + H_ROW : 32 * q + H_ROW + 4, :].bitcast(I32))
 
         pieces = [(n, s, 0, HALF) for n in range(N_TILES) for s in (1, 0)]
-        y_banks = (2, 6, 3, 7, 0, 4) * 2
+        y_banks = [PACK * s + t for s, t in groups] * 2
         res = [sb([P, S], F32, "y%d" % n) for n in range(N_TILES)]
         y_acc = {}
 
-        def direct(index):
+        def direct(index, a):
             n, s, lo, hi = pieces[index]
-            y_acc[index] = bank(y_banks[index], "y_acc%d" % index)
-            for a in range(PASSES):
-                scale = wd_sc[WD_ROW:P, N * a + P * n : N * a + P * (n + 1)]
-                times_v(y_acc[index], wd[:, a, P * n : P * (n + 1)].bitcast(FP8X4), scale, a, s, a == 0, False, lo, hi)
+            if a == 0:
+                y_acc[index] = bank(y_banks[index], "y_acc%d" % index)
+            scale = wd_sc[WD_ROW:P, N * a + P * n : N * a + P * (n + 1)]
+            times_v(y_acc[index], wd[:, a, P * n : P * (n + 1)].bitcast(FP8X4), scale, a, s, a == 0, False, lo, hi)
 
         def close(index):
             n, s, lo, hi = pieces[index]
@@ -294,9 +305,10 @@ def tile_list_branch_max_combining_kernel(
             if s == 0:
                 nc.sync.dma_start(out_0[cols, :], res[n][:])
 
-        for index in range(AHEAD):
-            direct(index)
+        passes = [(index, a) for index in range(len(pieces)) for a in range(PASSES)]
+        for index, a in passes[:AHEAD]:
+            direct(index, a)
         for index in range(len(pieces)):
-            if index >= AHEAD:
-                direct(index)
             close(index)
+            for later, a in passes[AHEAD + index : AHEAD + index + 1]:
+                direct(later, a)

@@ -27,15 +27,20 @@ N_TILES = N // P
 WY_CHUNK = 256
 QUADS = 4
 BANKS = 8
-QUARTER = HALF // 2
 WARM_UPS = 4
-AHEAD = 14
+AHEAD = 12
 SC_ROWS = 32
 WD_ROW = 4
 H_ROW = 8
-WA_BYTES = PACK * H * 4
-WY_BYTES = PACK * N * 4
-TAB_AT = (PASSES * WA_BYTES, PASSES * WA_BYTES + 2 * H + WY_BYTES)
+KB = 1024
+B_AT = 0
+WA_AT = (12 * KB, 20 * KB)
+TAB_SC_AT = 19 * KB
+TAB_AT = (28 * KB, 41 * KB)
+BF_AT = 49 * KB
+EARLY_GROUPS = 3
+SCALAR_TOKENS = 96
+LEAD = 4
 
 
 def tile_list_branch_max_combining_kernel(
@@ -47,8 +52,11 @@ def tile_list_branch_max_combining_kernel(
         placed = ctx.enter_context(tc.tile_pool(name="placed", bufs=1))
         psum = ctx.enter_context(tc.psum_pool(name="psum", bufs=1))
 
-        def sb(shape, dtype, name, tag=None):
-            return keep.tile(shape, dtype, name=name, tag=tag or name, align_bytes=64)
+        def sb(shape, dtype, name):
+            return keep.tile(shape, dtype, name=name, align_bytes=64)
+
+        def at(offset, shape, dtype, name):
+            return placed.tile(shape, dtype, name=name, offset=offset, align_bytes=64)
 
         def bank(index, name):
             return psum.tile([P, HALF], F32, name=name, tag="bank%d" % index)
@@ -60,240 +68,227 @@ def tile_list_branch_max_combining_kernel(
                 nc.vector.tensor_copy(out, in_)
 
         offsets = keep.tile([P, S // 16], U16, name="offsets")
-        tab_sc = sb([P, T], U8, "tab_sc")
-        wb_sc_raw = placed.tile([P, H], U8, name="wb_sc_raw", offset=WA_BYTES - H // 2)
-        planes = [sb([P, S + H], U8, "plane0")]
+        tab_sc = at(TAB_SC_AT, [P, T], U8, "tab_sc")
+        wb_sc_raw = at(TAB_AT[1], [P, H], U8, "wb_sc_raw")
         for lo, hi in ((SC_ROWS, 64), (64, P)):
-            nc.vector.memset(tab_sc[lo:hi, :].bitcast(I32), 0)
             nc.vector.memset(wb_sc_raw[lo:hi, :].bitcast(I32), 0)
+            nc.vector.memset(tab_sc[lo:hi, :].bitcast(I32), 0)
+        wb_planes = sb([P, PASSES * H], U8, "wb_planes")
+        v_planes = sb([P, PASSES * S], U8, "v_planes")
+        nc.vector.memset(wb_planes[:].bitcast(I32), 0)
+        nc.vector.memset(v_planes[:].bitcast(I32), 0)
         by_rows = sb([P, P], F32, "by_rows")
         nc.gpsimd.memset(by_rows[:], 0.0)
         identity = sb([P, P], F32, "identity")
         make_identity(nc, identity[:])
 
         def load_tab(a):
-            tile = placed.tile([P, T], I32, name="tab%d" % a, offset=TAB_AT[a])
+            tile = at(TAB_AT[a], [P, T], I32, "tab%d" % a)
             nc.sync.dma_start(tile[:], tab_words[a].rearrange("p t i -> p (t i)").bitcast(I32))
             return tile
 
         def load_scale_rows(tile, scales):
-            nc.sync.dma_start(tile[0:SC_ROWS].bitcast(I32), scales.rearrange("a q c -> (a q) c").bitcast(I32))
+            nc.sync.dma_start(tile[0:SC_ROWS].bitcast(I32), scales.bitcast(I32).rearrange("a q c -> q a c"))
 
+        def spread_rows(plane_tile, rows):
+            for q in (0, 2, 1, 3):
+                nc.sync.dma_start(plane_tile[32 * q : 32 * q + 4, :].bitcast(I32), rows[8 * q : 8 * q + 8, :].bitcast(I32))
+
+        load_scale_rows(wb_sc_raw[:], wb_scales)
         nc.sync.dma_start(offsets[:], offs)
         load_scale_rows(tab_sc[:], tab_scales)
-        load_scale_rows(wb_sc_raw[:], wb_scales)
         wb_raw = sb([P, PASSES, H // 2], I32, "wb_raw")
         nc.sync.dma_start(wb_raw[:], wb_words.bitcast(I32).rearrange("a p c -> p a c"))
         tab = [load_tab(0)]
         nc.sync.dma_start(by_rows[0:N_TILES, :], by.rearrange("(c p) -> c p", p=P))
+        wb_sc = sb([P, H], U8, "wb_sc")
+        nc.vector.tensor_copy(
+            wb_sc[:].rearrange("p (t m) -> p t m", t=PACK),
+            wb_sc_raw[:].rearrange("p (m t) -> p t m", t=PACK),
+        )
+        spread_rows(wb_planes, wb_sc)
         tab.append(load_tab(1))
+
+        def deal_wb(dealt, a):
+            nc.scalar.copy(
+                dealt[:].bitcast(U16).rearrange("p (t m) -> p t m", t=PACK),
+                wb_raw[:, a, :].bitcast(U16).rearrange("p (m t) -> p t m", t=PACK),
+            )
+            return dealt
+
+        wb = [deal_wb(sb([P, 2 * H], U8, "wb0"), 0)]
 
         by_cols = psum.tile([P, P], F32, name="by_cols", tag="bank%d" % (BANKS - 1))
         nc.tensor.transpose(by_cols[:], by_rows[:], identity[:])
         bias = sb([P, N_TILES], F32, "bias")
-        nc.scalar.activation(bias[:], by_cols[:, 0:N_TILES], COPY)
 
         v_sc = sb([P, S], U8, "v_sc")
         nc.vector.tensor_copy(v_sc[:], tab_sc[:].indirect(offsets[:]))
-        nc.vector.tensor_copy(planes[0][:, 0:S].bitcast(I32), v_sc[:].bitcast(I32))
-        nc.vector.tensor_copy(
-            planes[0][:, S : S + H].rearrange("p (t m) -> p t m", t=PACK),
-            wb_sc_raw[:].rearrange("p (m t) -> p t m", t=PACK),
-        )
-        planes.append(sb([P, S + H], U8, "plane1", "v_sc"))
-        nc.vector.memset(planes[1][:].bitcast(I32), 0)
+        spread_rows(v_planes, v_sc)
         wa_raw = []
-
-        def load_wa(a):
-            wa_raw.append(placed.tile([P, PACK, H], F32, name="wa_raw%d" % a, offset=WA_BYTES * a))
-            nc.sync.dma_start(wa_raw[a][:], wa[512 * a : 512 * (a + 1), :].rearrange("(p j) c -> p j c", j=PACK))
-
         for a in range(PASSES):
-            for q in range(QUADS):
-                row = 16 * a + 4 * q
-                if row > 0:
-                    nc.sync.dma_start(planes[a][32 * q : 32 * q + 4, :].bitcast(I32), planes[0][row : row + 4, :].bitcast(I32))
-            if a == 0:
-                load_wa(0)
+            wa_raw.append(at(WA_AT[a], [P, PACK, H], F32, "wa_raw%d" % a))
+            nc.sync.dma_start(wa_raw[a][:], wa[512 * a : 512 * (a + 1), :].rearrange("(p j) c -> p j c", j=PACK))
+        nc.scalar.activation(bias[:], by_cols[:, 0:N_TILES], COPY)
 
-        load_wa(1)
-        wb = []
         v = {}
         for a in range(PASSES):
-            if a == 0:
-                wb.append(sb([P, 2 * H], U8, "wb0"))
-            else:
-                wb.append(placed.tile([P, 2 * H], U8, name="wb1", offset=TAB_AT[0], align_bytes=64))
-            nc.vector.tensor_copy(
-                wb[a][:].bitcast(U16).rearrange("p (t m) -> p t m", t=PACK),
-                wb_raw[:, a, :].bitcast(U16).rearrange("p (m t) -> p t m", t=PACK),
-            )
             for s in range(HALVES):
                 v[a, s] = sb([P, HALF], U32, "v%d_%d" % (a, s))
                 cols = HALF // 16
                 nc.vector.tensor_copy(v[a, s][:], tab[a][:].bitcast(U32).indirect(offsets[:, cols * s : cols * (s + 1)]))
-
-        wd_sc = wb_raw[:].rearrange("p a c -> p (a c)")[:, 0 : PASSES * N // 4].bitcast(U8)
-        wd_rows = wd_scales.bitcast(I32).rearrange("a q c -> q a c")
-        for q in range(QUADS):
-            nc.sync.dma_start(
-                wd_sc[32 * q + WD_ROW : 32 * q + WD_ROW + 4, :].bitcast(I32).rearrange("p (a c) -> p a c", a=PASSES),
-                wd_rows[4 * q : 4 * q + 4],
-            )
-        wy_raw = placed.tile([P, PACK, N], F32, name="wy_raw", offset=TAB_AT[0] + 2 * H, align_bytes=64)
-        nc.sync.dma_start(wy_raw[:], wy.rearrange("(p j) n -> p j n", j=PACK))
-        wd = placed.tile([P, PASSES, N], I32, name="wd", offset=TAB_AT[1], align_bytes=64)
-        for a in range(PASSES):
-            nc.sync.dma_start(wd[:, a, :], wd_words[a].rearrange("p c i -> p (c i)").bitcast(I32))
 
         warm = bank(BANKS - 2, "warm")
         for index in range(WARM_UPS):
             nc.tensor.matmul_mx(
                 out=warm[:],
                 lhsT=tab[0][:, 0:P].bitcast(FP8X4),
-                lhsT_scale=tab_sc[:, 0:P],
+                lhsT_scale=wb_sc[:, 0:P],
                 rhs=tab[0][:, 0:HALF].bitcast(FP8X4),
-                rhs_scale=tab_sc[:, 0:HALF],
+                rhs_scale=wb_sc[:, 0:HALF],
                 start=True,
                 stop=True,
             )
 
-        def times_v(acc, lhsT, lhsT_scale, a, s, start, stop, lo=0, hi=HALF):
+        wy_raw = at(TAB_AT[0] + 2 * H, [P, PACK, N], F32, "wy_raw")
+        nc.sync.dma_start(wy_raw[:], wy.rearrange("(p j) n -> p j n", j=PACK))
+        wb.append(deal_wb(at(TAB_AT[0], [P, 2 * H], U8, "wb1"), 1))
+        wd_sc = wb_raw[:].rearrange("p a c -> p (a c)")[:, 0 : PASSES * N // 4].rearrange("p (a c) -> p a c", a=PASSES)
+        wd_rows = wd_scales.bitcast(I32).rearrange("a (q r) c -> r q a c", r=4)
+        for r in range(4):
+            nc.sync.dma_start(wd_sc[WD_ROW + r : P : 32], wd_rows[r])
+        wd = at(TAB_AT[1], [P, PASSES, N], I32, "wd")
+        for a in range(PASSES):
+            nc.sync.dma_start(wd[:, a, :], wd_words[a].rearrange("p c i -> p (c i)").bitcast(I32))
+
+        def times_v(acc, lhsT, lhsT_scale, a, s, start, stop):
             nc.tensor.matmul_mx(
-                out=acc[:, 0 : hi - lo],
+                out=acc[:],
                 lhsT=lhsT,
                 lhsT_scale=lhsT_scale,
-                rhs=v[a, s][:, lo:hi].bitcast(FP8X4),
-                rhs_scale=planes[a][:, HALF * s + lo : HALF * s + hi],
+                rhs=v[a, s][:].bitcast(FP8X4),
+                rhs_scale=v_planes[:, S * a + HALF * s : S * a + HALF * (s + 1)],
                 start=start,
                 stop=stop,
             )
 
-        def branch_b(acc, a, s, t):
-            times_v(
-                acc,
-                wb[a][:, 2 * P * t : 2 * P * (t + 1)].bitcast(FP4X4),
-                planes[a][:, S + P * t : S + P * (t + 1)],
-                a, s, a == 0, a == PASSES - 1,
-            )
-
-        def branch_a(acc, a, s, t):
-            codes = wa_q[a, t // 2][:, P * (t % 2) : P * (t % 2 + 1)].bitcast(FP8X4)
-            times_v(acc, codes, wa_sc[:, a, P * t : P * (t + 1)], a, s, a == 0, a == PASSES - 1)
-
-        b_acc = {(s, t): bank(PACK * s + t, "b_acc%d_%d" % (s, t)) for s in range(HALVES) for t in range(PACK)}
         groups = [(s, t) for t in range(2) for s in range(HALVES)]
         groups += [(s, t) for s in range(HALVES) for t in range(2, PACK)]
+        b_acc = {group: bank(index, "b_acc%d" % index) for index, group in enumerate(groups)}
         for a in range(PASSES):
             for s, t in sorted(groups):
-                branch_b(b_acc[s, t], a, s, t)
+                times_v(
+                    b_acc[s, t],
+                    wb[a][:, 2 * P * t : 2 * P * (t + 1)].bitcast(FP4X4),
+                    wb_planes[:, H * a + P * t : H * a + P * (t + 1)],
+                    a, s, a == 0, a == PASSES - 1,
+                )
 
         wa_q = {}
-        wa_sc = sb([P, PASSES, H], U8, "wa_sc")
-        wa_bf = {}
+        wa_sc = {}
 
-        def round_wa(engine, a, u):
-            wa_bf[a, u] = sb([P, 2 * P * PACK], BF16, "wa_bf%d_%d" % (a, u))
+        def quantize_wa(engine, a, t, slots):
+            rounded = sb([P, slots * P * PACK], BF16, "wa_bf%d_%d" % (a, t))
             cast(
                 engine,
-                wa_bf[a, u][:].rearrange("p (t m j) -> p m j t", t=2, j=PACK),
-                wa_raw[a][:].rearrange("p j (m t) -> p m j t", t=PACK)[:, :, :, 2 * u : 2 * u + 2],
+                rounded[:].rearrange("p (t m j) -> p m j t", t=slots, j=PACK),
+                wa_raw[a][:].rearrange("p j (m t) -> p m j t", t=PACK)[:, :, :, t : t + slots],
             )
+            codes = sb([P, slots * P], U32, "wa_q%d_%d" % (a, t))
+            scales = sb([P, slots * P], U8, "wa_sc%d_%d" % (a, t))
+            nc.vector.quantize_mx(out=codes[:].bitcast(FP8X4), scales=scales[:], in_=rounded[:])
+            for u in range(slots):
+                wa_q[a, t + u] = codes[:, P * u : P * (u + 1)].bitcast(FP8X4)
+                wa_sc[a, t + u] = scales[:, P * u : P * (u + 1)]
 
-        def quantize_wa(a, u, tag=None):
-            wa_q[a, u] = sb([P, 2 * P], U32, "wa_q%d_%d" % (a, u), tag)
-            cols = slice(2 * P * u, 2 * P * (u + 1))
-            nc.vector.quantize_mx(out=wa_q[a, u][:].bitcast(FP8X4), scales=wa_sc[:, a, cols], in_=wa_bf[a, u][:])
+        quantize_wa("scalar", 0, 0, 2)
+        quantize_wa("vector", 0, 2, 2)
+        quantize_wa("vector", 1, 0, 2)
+        quantize_wa("vector", 1, 2, 2)
 
-        round_wa("scalar", 0, 0)
-        round_wa("vector", 0, 1)
-        quantize_wa(0, 0)
-        round_wa("vector", 1, 0)
-        round_wa("vector", 1, 1)
-        quantize_wa(1, 0)
-        quantize_wa(0, 1, "wa_bf1_0")
-        quantize_wa(1, 1)
-
-        b_sb = {}
-        for s, t in groups:
-            b_sb[s, t] = sb([P, HALF], F32, "b_sb%d_%d" % (s, t))[:]
-            nc.scalar.activation(b_sb[s, t], b_acc[s, t][:], COPY)
+        b_tile = at(B_AT, [P, BANKS, HALF], F32, "b_sb")
+        b_sb = {group: b_tile[:, index, :] for index, group in enumerate(groups)}
+        for group in groups:
+            nc.scalar.activation(b_sb[group], b_acc[group][:], COPY)
 
         h = sb([P, PACK, S], F32, "h")
         h_out = out_1.rearrange("(p t) j -> p t j", t=PACK)
-        for s, t in groups:
-            a_acc = bank(PACK * s + t, "a_acc%d_%d" % (s, t))
-            for a in range(PASSES):
-                branch_a(a_acc, a, s, t)
+        for index, (s, t) in enumerate(groups):
+            a_acc = bank(index, "a_acc%d" % index)
+            order = (0, 1) if index < EARLY_GROUPS else (1, 0)
+            for a in order:
+                times_v(a_acc, wa_q[a, t], wa_sc[a, t], a, s, a == order[0], a == order[1])
             nc.vector.tensor_tensor(h[:, t, HALF * s : HALF * (s + 1)], a_acc[:], b_sb[s, t], MAX)
             if s == HALVES - 1:
                 nc.sync.dma_start(h_out[:, t, :], h[:, t, :])
 
         wy_q = sb([P, N], U32, "wy_q")
         wy_sc = sb([P, N], U8, "wy_sc")
-        wy_bf = [sb([P, WY_CHUNK * PACK], BF16, "wy_bf%d" % c)[:] for c in range(N // WY_CHUNK)]
 
-        def round_wy(engine, c):
+        def round_wy(engine, rounded, c):
             cast(
                 engine,
-                wy_bf[c].rearrange("p (c i j) -> p c j i", i=4, j=PACK),
+                rounded.rearrange("p (c i j) -> p c j i", i=4, j=PACK),
                 wy_raw[:, :, WY_CHUNK * c : WY_CHUNK * (c + 1)].rearrange("p j (c i) -> p c j i", i=4),
             )
 
-        def quantize_wy(c):
+        def quantize_wy(rounded, c):
             cols = slice(WY_CHUNK * c, WY_CHUNK * (c + 1))
-            nc.vector.quantize_mx(out=wy_q[:, cols].bitcast(FP8X4), scales=wy_sc[:, cols], in_=wy_bf[c])
-
-        h_q = sb([P, S], U32, "h_q")
-        h_sc = sb([P, S], U8, "h_sc")
-        words_out = out_2[0].rearrange("p m t -> p (m t)").bitcast(I32)
+            nc.vector.quantize_mx(out=wy_q[:, cols].bitcast(FP8X4), scales=wy_sc[:, cols], in_=rounded)
 
         def round_h(engine, rounded, lo, hi):
-            cast(
-                engine,
-                rounded.rearrange("p (c i t) -> p c t i", i=4, t=PACK),
-                h[:, :, lo:hi].rearrange("p t (c i) -> p c t i", i=4),
-            )
+            if hi <= HALF:
+                cast(engine, rounded.rearrange("p (c t) -> p c t", t=PACK), h[:, :, lo:hi].rearrange("p t c -> p c t"))
+            else:
+                cast(
+                    engine,
+                    rounded.rearrange("p (c i t) -> p c t i", i=4, t=PACK),
+                    h[:, :, lo:hi].rearrange("p t (c i) -> p c t i", i=4),
+                )
 
         def quantize_h(rounded, lo, hi):
             nc.vector.quantize_mx(out=h_q[:, lo:hi].bitcast(FP8X4), scales=h_sc[H_ROW:P, lo:hi], in_=rounded)
 
-        round_wy("scalar", 0)
-        round_wy("scalar", 1)
-        quantize_wy(0)
-        quarters = [wy_raw[:, j, 0 : 2 * WY_CHUNK].bitcast(BF16) for j in range(2)]
-        for j in range(2):
-            round_h("scalar", quarters[j], QUARTER * j, QUARTER * (j + 1))
-        second = sb([P, HALF * PACK], BF16, "h_bf1", "wy_bf0")
-        round_h("vector", second[:], HALF, S)
+        h_q = sb([P, S], U32, "h_q")
+        h_sc = sb([P, S], U8, "h_sc")
+        wy_bf0 = at(BF_AT, [P, WY_CHUNK * PACK], BF16, "wy_bf0")
+        round_wy("scalar", wy_bf0[:], 0)
+        quantize_wy(wy_bf0[:], 0)
+        eighths = [wy_raw[:, j, 0:WY_CHUNK].bitcast(BF16) for j in range(PACK)]
+        for j in range(PACK):
+            round_h("scalar", eighths[j], P * j, P * (j + 1))
+        second = at(BF_AT, [P, HALF * PACK], BF16, "second")
+        cut = HALF - SCALAR_TOKENS
+        round_h("vector", second[:, 0 : PACK * cut], HALF, HALF + cut)
+        round_h("scalar", second[:, PACK * cut :], HALF + cut, S)
+        for j in range(PACK):
+            quantize_h(eighths[j], P * j, P * (j + 1))
         quantize_h(second[:], HALF, S)
-        for j in range(2):
-            quantize_h(quarters[j], QUARTER * j, QUARTER * (j + 1))
-        nc.sync.dma_start(words_out, h_q[:].bitcast(I32))
-        quantize_wy(1)
-        round_wy("vector", 2)
-        quantize_wy(2)
+        nc.sync.dma_start(out_2[0].rearrange("p m t -> p (m t)").bitcast(I32), h_q[:].bitcast(I32))
+        for c in (1, 2):
+            rounded = at(BF_AT + 2 * KB * (c - 1), [P, WY_CHUNK * PACK], BF16, "wy_bf%d" % c)
+            round_wy("vector", rounded[:], c)
+            quantize_wy(rounded[:], c)
         for q in range(QUADS):
-            nc.sync.dma_start(out_3[0, 4 * q : 4 * q + 4, :].bitcast(I32), h_sc[32 * q + H_ROW : 32 * q + H_ROW + 4, :].bitcast(I32))
+            nc.sync.dma_start(out_3[0, q : 16 : 4, :].bitcast(I32), h_sc[H_ROW + q : P : 32, :].bitcast(I32))
 
-        pieces = [(n, s, 0, HALF) for n in range(N_TILES) for s in (1, 0)]
-        y_banks = [PACK * s + t for s, t in groups] * 2
+        pieces = [(n, s) for n in range(N_TILES) for s in range(HALVES)]
         res = [sb([P, S], F32, "y%d" % n) for n in range(N_TILES)]
         y_acc = {}
 
         def direct(index, a):
-            n, s, lo, hi = pieces[index]
+            n, s = pieces[index]
             if a == 0:
-                y_acc[index] = bank(y_banks[index], "y_acc%d" % index)
-            scale = wd_sc[WD_ROW:P, N * a + P * n : N * a + P * (n + 1)]
-            times_v(y_acc[index], wd[:, a, P * n : P * (n + 1)].bitcast(FP8X4), scale, a, s, a == 0, False, lo, hi)
+                y_acc[index] = bank(index % BANKS, "y_acc%d" % index)
+            cols = slice(P * n, P * (n + 1))
+            times_v(y_acc[index], wd[:, a, cols].bitcast(FP8X4), wd_sc[WD_ROW:P, a, :].bitcast(U8)[:, cols], a, s, a == 0, False)
 
         def close(index):
-            n, s, lo, hi = pieces[index]
+            n, s = pieces[index]
             cols = slice(P * n, P * (n + 1))
-            tokens = slice(HALF * s + lo, HALF * s + hi)
+            tokens = slice(HALF * s, HALF * (s + 1))
             nc.tensor.matmul_mx(
-                out=y_acc[index][:, 0 : hi - lo],
+                out=y_acc[index][:],
                 lhsT=wy_q[:, cols].bitcast(FP8X4),
                 lhsT_scale=wy_sc[:, cols],
                 rhs=h_q[:, tokens].bitcast(FP8X4),
@@ -301,14 +296,18 @@ def tile_list_branch_max_combining_kernel(
                 start=False,
                 stop=True,
             )
-            nc.scalar.activation(res[n][:, tokens], y_acc[index][:, 0 : hi - lo], TANH, bias=bias[:, n : n + 1])
-            if s == 0:
+            nc.scalar.activation(res[n][:, tokens], y_acc[index][:], TANH, bias=bias[:, n : n + 1])
+            if n == N_TILES - 1:
+                nc.sync.dma_start(out_0[cols, tokens], res[n][:, tokens])
+            elif s == HALVES - 1:
                 nc.sync.dma_start(out_0[cols, :], res[n][:])
 
-        passes = [(index, a) for index in range(len(pieces)) for a in range(PASSES)]
-        for index, a in passes[:AHEAD]:
-            direct(index, a)
+        passes = [(index, a) for a in range(PASSES) for index in range(LEAD)]
+        passes += [(index, a) for index in range(LEAD, len(pieces)) for a in range(PASSES)]
+        done = 0
         for index in range(len(pieces)):
-            close(index)
-            for later, a in passes[AHEAD + index : AHEAD + index + 1]:
+            upto = max(AHEAD + index, PASSES * (index + 1))
+            for later, a in passes[done:upto]:
                 direct(later, a)
+            done = upto
+            close(index)

@@ -24,21 +24,21 @@ PASSES = K // (P * PACK)
 HALF = 512
 HALVES = S // HALF
 N_TILES = N // P
-WY_CHUNK = 256
 QUADS = 4
 BANKS = 8
 WARM_UPS = 4
-AHEAD = 12
+AHEAD = 11
 SC_ROWS = 32
 WD_ROW = 4
 H_ROW = 8
 KB = 1024
 B_AT = 0
 WA_AT = (12 * KB, 20 * KB)
-TAB_SC_AT = 19 * KB
+V_SC_AT = 19 * KB + 512
 TAB_AT = (28 * KB, 41 * KB)
-BF_AT = 49 * KB
+BF_AT = 50 * KB
 EARLY_GROUPS = 3
+Y_BANKS = 6
 SCALAR_TOKENS = 96
 LEAD = 4
 
@@ -68,15 +68,13 @@ def tile_list_branch_max_combining_kernel(
                 nc.vector.tensor_copy(out, in_)
 
         offsets = keep.tile([P, S // 16], U16, name="offsets")
-        tab_sc = at(TAB_SC_AT, [P, T], U8, "tab_sc")
-        wb_sc_raw = at(TAB_AT[1], [P, H], U8, "wb_sc_raw")
+        tab_sc = sb([P, T], U8, "tab_sc")
+        wb_sc_raw = sb([P, H], U8, "wb_sc_raw")
         for lo, hi in ((SC_ROWS, 64), (64, P)):
             nc.vector.memset(wb_sc_raw[lo:hi, :].bitcast(I32), 0)
             nc.vector.memset(tab_sc[lo:hi, :].bitcast(I32), 0)
-        wb_planes = sb([P, PASSES * H], U8, "wb_planes")
-        v_planes = sb([P, PASSES * S], U8, "v_planes")
-        nc.vector.memset(wb_planes[:].bitcast(I32), 0)
-        nc.vector.memset(v_planes[:].bitcast(I32), 0)
+        planes = [sb([P, S + H], U8, "plane%d" % a) for a in range(PASSES)]
+        nc.vector.memset(planes[1][:].bitcast(I32), 0)
         by_rows = sb([P, P], F32, "by_rows")
         nc.gpsimd.memset(by_rows[:], 0.0)
         identity = sb([P, P], F32, "identity")
@@ -88,11 +86,7 @@ def tile_list_branch_max_combining_kernel(
             return tile
 
         def load_scale_rows(tile, scales):
-            nc.sync.dma_start(tile[0:SC_ROWS].bitcast(I32), scales.bitcast(I32).rearrange("a q c -> q a c"))
-
-        def spread_rows(plane_tile, rows):
-            for q in (0, 2, 1, 3):
-                nc.sync.dma_start(plane_tile[32 * q : 32 * q + 4, :].bitcast(I32), rows[8 * q : 8 * q + 8, :].bitcast(I32))
+            nc.sync.dma_start(tile[0:SC_ROWS].bitcast(I32), scales.bitcast(I32).rearrange("a q c -> (a q) c"))
 
         load_scale_rows(wb_sc_raw[:], wb_scales)
         nc.sync.dma_start(offsets[:], offs)
@@ -101,12 +95,10 @@ def tile_list_branch_max_combining_kernel(
         nc.sync.dma_start(wb_raw[:], wb_words.bitcast(I32).rearrange("a p c -> p a c"))
         tab = [load_tab(0)]
         nc.sync.dma_start(by_rows[0:N_TILES, :], by.rearrange("(c p) -> c p", p=P))
-        wb_sc = sb([P, H], U8, "wb_sc")
         nc.vector.tensor_copy(
-            wb_sc[:].rearrange("p (t m) -> p t m", t=PACK),
+            planes[0][:, S : S + H].rearrange("p (t m) -> p t m", t=PACK),
             wb_sc_raw[:].rearrange("p (m t) -> p t m", t=PACK),
         )
-        spread_rows(wb_planes, wb_sc)
         tab.append(load_tab(1))
 
         def deal_wb(dealt, a):
@@ -122,11 +114,18 @@ def tile_list_branch_max_combining_kernel(
         nc.tensor.transpose(by_cols[:], by_rows[:], identity[:])
         bias = sb([P, N_TILES], F32, "bias")
 
-        v_sc = sb([P, S], U8, "v_sc")
+        v_sc = at(V_SC_AT, [P, S], U8, "v_sc")
         nc.vector.tensor_copy(v_sc[:], tab_sc[:].indirect(offsets[:]))
-        spread_rows(v_planes, v_sc)
+        nc.vector.tensor_copy(planes[0][:, 0:S].bitcast(I32), v_sc[:].bitcast(I32))
+        rows = [plane[:].bitcast(I32) for plane in planes]
         wa_raw = []
         for a in range(PASSES):
+            if a == 0:
+                for q in (2, 1, 3):
+                    nc.sync.dma_start(rows[0][32 * q : 32 * q + 4], rows[0][4 * q : 4 * q + 4])
+            else:
+                for r in range(4):
+                    nc.sync.dma_start(rows[1][r:P:32], rows[0][16 + r : 32 : 4])
             wa_raw.append(at(WA_AT[a], [P, PACK, H], F32, "wa_raw%d" % a))
             nc.sync.dma_start(wa_raw[a][:], wa[512 * a : 512 * (a + 1), :].rearrange("(p j) c -> p j c", j=PACK))
         nc.scalar.activation(bias[:], by_cols[:, 0:N_TILES], COPY)
@@ -143,9 +142,9 @@ def tile_list_branch_max_combining_kernel(
             nc.tensor.matmul_mx(
                 out=warm[:],
                 lhsT=tab[0][:, 0:P].bitcast(FP8X4),
-                lhsT_scale=wb_sc[:, 0:P],
+                lhsT_scale=tab_sc[:, 0:P],
                 rhs=tab[0][:, 0:HALF].bitcast(FP8X4),
-                rhs_scale=wb_sc[:, 0:HALF],
+                rhs_scale=tab_sc[:, 0:HALF],
                 start=True,
                 stop=True,
             )
@@ -167,7 +166,7 @@ def tile_list_branch_max_combining_kernel(
                 lhsT=lhsT,
                 lhsT_scale=lhsT_scale,
                 rhs=v[a, s][:].bitcast(FP8X4),
-                rhs_scale=v_planes[:, S * a + HALF * s : S * a + HALF * (s + 1)],
+                rhs_scale=planes[a][:, HALF * s : HALF * (s + 1)],
                 start=start,
                 stop=stop,
             )
@@ -176,11 +175,11 @@ def tile_list_branch_max_combining_kernel(
         groups += [(s, t) for s in range(HALVES) for t in range(2, PACK)]
         b_acc = {group: bank(index, "b_acc%d" % index) for index, group in enumerate(groups)}
         for a in range(PASSES):
-            for s, t in sorted(groups):
+            for s, t in sorted(groups) if a == 0 else groups:
                 times_v(
                     b_acc[s, t],
                     wb[a][:, 2 * P * t : 2 * P * (t + 1)].bitcast(FP4X4),
-                    wb_planes[:, H * a + P * t : H * a + P * (t + 1)],
+                    planes[a][:, S + P * t : S + P * (t + 1)],
                     a, s, a == 0, a == PASSES - 1,
                 )
 
@@ -222,19 +221,20 @@ def tile_list_branch_max_combining_kernel(
             if s == HALVES - 1:
                 nc.sync.dma_start(h_out[:, t, :], h[:, t, :])
 
-        wy_q = sb([P, N], U32, "wy_q")
+        wy_q = {}
         wy_sc = sb([P, N], U8, "wy_sc")
 
-        def round_wy(engine, rounded, c):
+        def round_wy(engine, rounded, first, tiles):
             cast(
                 engine,
                 rounded.rearrange("p (c i j) -> p c j i", i=4, j=PACK),
-                wy_raw[:, :, WY_CHUNK * c : WY_CHUNK * (c + 1)].rearrange("p j (c i) -> p c j i", i=4),
+                wy_raw[:, :, P * first : P * (first + tiles)].rearrange("p j (c i) -> p c j i", i=4),
             )
 
-        def quantize_wy(rounded, c):
-            cols = slice(WY_CHUNK * c, WY_CHUNK * (c + 1))
-            nc.vector.quantize_mx(out=wy_q[:, cols].bitcast(FP8X4), scales=wy_sc[:, cols], in_=rounded)
+        def quantize_wy(codes, rounded, first, tiles):
+            nc.vector.quantize_mx(out=codes[:].bitcast(FP8X4), scales=wy_sc[:, P * first : P * (first + tiles)], in_=rounded)
+            for n in range(tiles):
+                wy_q[first + n] = codes[:, P * n : P * (n + 1)].bitcast(FP8X4)
 
         def round_h(engine, rounded, lo, hi):
             if hi <= HALF:
@@ -251,10 +251,12 @@ def tile_list_branch_max_combining_kernel(
 
         h_q = sb([P, S], U32, "h_q")
         h_sc = sb([P, S], U8, "h_sc")
-        wy_bf0 = at(BF_AT, [P, WY_CHUNK * PACK], BF16, "wy_bf0")
-        round_wy("scalar", wy_bf0[:], 0)
-        quantize_wy(wy_bf0[:], 0)
-        eighths = [wy_raw[:, j, 0:WY_CHUNK].bitcast(BF16) for j in range(PACK)]
+        wy_bf0 = at(BF_AT, [P, P * PACK], BF16, "wy_bf0")
+        wy_bf1 = sb([P, P * PACK], BF16, "wy_bf1")
+        round_wy("scalar", wy_bf0[:], 0, 1)
+        round_wy("scalar", wy_bf1[:], 1, 1)
+        quantize_wy(sb([P, P], U32, "wy_q0"), wy_bf0[:], 0, 1)
+        eighths = [wy_raw[:, j, 0 : 2 * P].bitcast(BF16) for j in range(PACK)]
         for j in range(PACK):
             round_h("scalar", eighths[j], P * j, P * (j + 1))
         second = at(BF_AT, [P, HALF * PACK], BF16, "second")
@@ -263,12 +265,15 @@ def tile_list_branch_max_combining_kernel(
         round_h("scalar", second[:, PACK * cut :], HALF + cut, S)
         for j in range(PACK):
             quantize_h(eighths[j], P * j, P * (j + 1))
+        words_out = out_2[0].rearrange("p m t -> p (m t)").bitcast(I32)
+        nc.sync.dma_start(words_out[:, 0:HALF], h_q[:, 0:HALF].bitcast(I32))
         quantize_h(second[:], HALF, S)
-        nc.sync.dma_start(out_2[0].rearrange("p m t -> p (m t)").bitcast(I32), h_q[:].bitcast(I32))
-        for c in (1, 2):
-            rounded = at(BF_AT + 2 * KB * (c - 1), [P, WY_CHUNK * PACK], BF16, "wy_bf%d" % c)
-            round_wy("vector", rounded[:], c)
-            quantize_wy(rounded[:], c)
+        nc.sync.dma_start(words_out[:, HALF:S], h_q[:, HALF:S].bitcast(I32))
+        quantize_wy(at(BF_AT + KB, [P, P], U32, "wy_q1"), wy_bf1[:], 1, 1)
+        for first, offset in ((2, BF_AT - KB), (4, BF_AT + 3 * KB)):
+            rounded = at(offset, [P, 2 * P * PACK], BF16, "wy_bf%d" % first)
+            round_wy("vector", rounded[:], first, 2)
+            quantize_wy(sb([P, 2 * P], U32, "wy_q%d" % first), rounded[:], first, 2)
         for q in range(QUADS):
             nc.sync.dma_start(out_3[0, q : 16 : 4, :].bitcast(I32), h_sc[H_ROW + q : P : 32, :].bitcast(I32))
 
@@ -279,7 +284,7 @@ def tile_list_branch_max_combining_kernel(
         def direct(index, a):
             n, s = pieces[index]
             if a == 0:
-                y_acc[index] = bank(index % BANKS, "y_acc%d" % index)
+                y_acc[index] = bank(index % Y_BANKS, "y_acc%d" % index)
             cols = slice(P * n, P * (n + 1))
             times_v(y_acc[index], wd[:, a, cols].bitcast(FP8X4), wd_sc[WD_ROW:P, a, :].bitcast(U8)[:, cols], a, s, a == 0, False)
 
@@ -289,7 +294,7 @@ def tile_list_branch_max_combining_kernel(
             tokens = slice(HALF * s, HALF * (s + 1))
             nc.tensor.matmul_mx(
                 out=y_acc[index][:],
-                lhsT=wy_q[:, cols].bitcast(FP8X4),
+                lhsT=wy_q[n],
                 lhsT_scale=wy_sc[:, cols],
                 rhs=h_q[:, tokens].bitcast(FP8X4),
                 rhs_scale=h_sc[H_ROW:P, tokens],

@@ -32,6 +32,7 @@ SC_ROWS = 32
 WD_ROW = 4
 H_ROW = 8
 KB = 1024
+ALIGN = 256
 B_AT = 0
 WA_AT = (12 * KB, 20 * KB)
 V_SC_AT = 19 * KB + 512
@@ -53,10 +54,10 @@ def tile_list_branch_max_combining_kernel(
         psum = ctx.enter_context(tc.psum_pool(name="psum", bufs=1))
 
         def sb(shape, dtype, name):
-            return keep.tile(shape, dtype, name=name, align_bytes=64)
+            return keep.tile(shape, dtype, name=name, align_bytes=ALIGN)
 
         def at(offset, shape, dtype, name):
-            return placed.tile(shape, dtype, name=name, offset=offset, align_bytes=64)
+            return placed.tile(shape, dtype, name=name, offset=offset, align_bytes=ALIGN)
 
         def bank(index, name):
             return psum.tile([P, HALF], F32, name=name, tag="bank%d" % index)
@@ -67,7 +68,7 @@ def tile_list_branch_max_combining_kernel(
             else:
                 nc.vector.tensor_copy(out, in_)
 
-        offsets = keep.tile([P, S // 16], U16, name="offsets")
+        offsets = keep.tile([P, S // 16], U16, name="offsets", align_bytes=ALIGN)
         tab_sc = sb([P, T], U8, "tab_sc")
         wb_sc_raw = sb([P, H], U8, "wb_sc_raw")
         for lo, hi in ((SC_ROWS, 64), (64, P)):
@@ -265,10 +266,8 @@ def tile_list_branch_max_combining_kernel(
         round_h("scalar", second[:, PACK * cut :], HALF + cut, S)
         for j in range(PACK):
             quantize_h(eighths[j], P * j, P * (j + 1))
-        words_out = out_2[0].rearrange("p m t -> p (m t)").bitcast(I32)
-        nc.sync.dma_start(words_out[:, 0:HALF], h_q[:, 0:HALF].bitcast(I32))
         quantize_h(second[:], HALF, S)
-        nc.sync.dma_start(words_out[:, HALF:S], h_q[:, HALF:S].bitcast(I32))
+        nc.sync.dma_start(out_2[0].rearrange("p m t -> p (m t)").bitcast(I32), h_q[:].bitcast(I32))
         quantize_wy(at(BF_AT + KB, [P, P], U32, "wy_q1"), wy_bf1[:], 1, 1)
         for first, offset in ((2, BF_AT - KB), (4, BF_AT + 3 * KB)):
             rounded = at(offset, [P, 2 * P * PACK], BF16, "wy_bf%d" % first)
@@ -302,9 +301,7 @@ def tile_list_branch_max_combining_kernel(
                 stop=True,
             )
             nc.scalar.activation(res[n][:, tokens], y_acc[index][:], TANH, bias=bias[:, n : n + 1])
-            if n == N_TILES - 1:
-                nc.sync.dma_start(out_0[cols, tokens], res[n][:, tokens])
-            elif s == HALVES - 1:
+            if s == HALVES - 1:
                 nc.sync.dma_start(out_0[cols, :], res[n][:])
 
         passes = [(index, a) for a in range(PASSES) for index in range(LEAD)]

@@ -27,7 +27,7 @@ N_TILES = N // P
 QUADS = 4
 BANKS = 8
 WARM_UPS = 4
-AHEAD = 11
+AHEAD = 12
 SC_ROWS = 32
 WD_ROW = 4
 H_ROW = 8
@@ -39,7 +39,7 @@ V_SC_AT = 19 * KB + 512
 TAB_AT = (28 * KB, 41 * KB)
 BF_AT = 50 * KB
 EARLY_GROUPS = 3
-Y_BANKS = 6
+Y_BANKS = 8
 SCALAR_TOKENS = 96
 LEAD = 4
 
@@ -301,7 +301,9 @@ def tile_list_branch_max_combining_kernel(
                 stop=True,
             )
             nc.scalar.activation(res[n][:, tokens], y_acc[index][:], TANH, bias=bias[:, n : n + 1])
-            if s == HALVES - 1:
+            if n == N_TILES - 1:
+                nc.sync.dma_start(out_0[cols, tokens], res[n][:, tokens])
+            elif s == HALVES - 1:
                 nc.sync.dma_start(out_0[cols, :], res[n][:])
 
         passes = [(index, a) for a in range(PASSES) for index in range(LEAD)]

@@ -40,7 +40,7 @@ TAB_AT = (28 * KB, 41 * KB)
 BF_AT = 50 * KB
 EARLY_GROUPS = 3
 Y_BANKS = 8
-SCALAR_TOKENS = 96
+SCALAR_TOKENS = 128
 LEAD = 4
 
 
@@ -74,8 +74,10 @@ def tile_list_branch_max_combining_kernel(
         for lo, hi in ((SC_ROWS, 64), (64, P)):
             nc.vector.memset(wb_sc_raw[lo:hi, :].bitcast(I32), 0)
             nc.vector.memset(tab_sc[lo:hi, :].bitcast(I32), 0)
-        planes = [sb([P, S + H], U8, "plane%d" % a) for a in range(PASSES)]
-        nc.vector.memset(planes[1][:].bitcast(I32), 0)
+        joined = sb([P, S + H], U8, "joined")
+        both = sb([P, PASSES * (S + H)], U8, "planes")
+        nc.vector.memset(both[:].bitcast(I32), 0)
+        planes = [both[:, (S + H) * a : (S + H) * (a + 1)] for a in range(PASSES)]
         by_rows = sb([P, P], F32, "by_rows")
         nc.gpsimd.memset(by_rows[:], 0.0)
         identity = sb([P, P], F32, "identity")
@@ -87,7 +89,7 @@ def tile_list_branch_max_combining_kernel(
             return tile
 
         def load_scale_rows(tile, scales):
-            nc.sync.dma_start(tile[0:SC_ROWS].bitcast(I32), scales.bitcast(I32).rearrange("a q c -> (a q) c"))
+            nc.sync.dma_start(tile[0:SC_ROWS].bitcast(I32), scales.bitcast(I32).rearrange("a q c -> q a c"))
 
         load_scale_rows(wb_sc_raw[:], wb_scales)
         nc.sync.dma_start(offsets[:], offs)
@@ -97,7 +99,7 @@ def tile_list_branch_max_combining_kernel(
         tab = [load_tab(0)]
         nc.sync.dma_start(by_rows[0:N_TILES, :], by.rearrange("(c p) -> c p", p=P))
         nc.vector.tensor_copy(
-            planes[0][:, S : S + H].rearrange("p (t m) -> p t m", t=PACK),
+            joined[:, S : S + H].rearrange("p (t m) -> p t m", t=PACK),
             wb_sc_raw[:].rearrange("p (m t) -> p t m", t=PACK),
         )
         tab.append(load_tab(1))
@@ -117,16 +119,11 @@ def tile_list_branch_max_combining_kernel(
 
         v_sc = at(V_SC_AT, [P, S], U8, "v_sc")
         nc.vector.tensor_copy(v_sc[:], tab_sc[:].indirect(offsets[:]))
-        nc.vector.tensor_copy(planes[0][:, 0:S].bitcast(I32), v_sc[:].bitcast(I32))
-        rows = [plane[:].bitcast(I32) for plane in planes]
+        nc.vector.tensor_copy(joined[:, 0:S].bitcast(I32), v_sc[:].bitcast(I32))
+        for q in (0, 2, 1, 3):
+            nc.sync.dma_start(both[32 * q : 32 * q + 4, :].bitcast(I32), joined[8 * q : 8 * q + 8, :].bitcast(I32))
         wa_raw = []
         for a in range(PASSES):
-            if a == 0:
-                for q in (2, 1, 3):
-                    nc.sync.dma_start(rows[0][32 * q : 32 * q + 4], rows[0][4 * q : 4 * q + 4])
-            else:
-                for r in range(4):
-                    nc.sync.dma_start(rows[1][r:P:32], rows[0][16 + r : 32 : 4])
             wa_raw.append(at(WA_AT[a], [P, PACK, H], F32, "wa_raw%d" % a))
             nc.sync.dma_start(wa_raw[a][:], wa[512 * a : 512 * (a + 1), :].rearrange("(p j) c -> p j c", j=PACK))
         nc.scalar.activation(bias[:], by_cols[:, 0:N_TILES], COPY)
@@ -172,8 +169,7 @@ def tile_list_branch_max_combining_kernel(
                 stop=stop,
             )
 
-        groups = [(s, t) for t in range(2) for s in range(HALVES)]
-        groups += [(s, t) for s in range(HALVES) for t in range(2, PACK)]
+        groups = [(0, 0), (1, 0)] + [(s, t) for s in range(HALVES) for t in range(1, PACK)]
         b_acc = {group: bank(index, "b_acc%d" % index) for index, group in enumerate(groups)}
         for a in range(PASSES):
             for s, t in sorted(groups) if a == 0 else groups:

@@ -17,6 +17,8 @@ FP4X4 = mybir.dt.float4_e2m1fn_x4
 COPY = mybir.ActivationFunctionType.Copy
 TANH = mybir.ActivationFunctionType.Tanh
 MAX = mybir.AluOpType.max
+MULT = mybir.AluOpType.mult
+ADD = mybir.AluOpType.add
 
 P = 128
 PACK = 4
@@ -26,8 +28,8 @@ HALVES = S // HALF
 N_TILES = N // P
 QUADS = 4
 BANKS = 8
-WARM_UPS = 4
-AHEAD = 12
+WARM_UPS = 6
+AHEAD = 11
 SC_ROWS = 32
 WD_ROW = 4
 H_ROW = 8
@@ -40,7 +42,7 @@ TAB_AT = (28 * KB, 41 * KB)
 BF_AT = 50 * KB
 EARLY_GROUPS = 3
 Y_BANKS = 8
-SCALAR_TOKENS = 128
+SCALAR_TOKENS = 176
 LEAD = 4
 
 
@@ -65,6 +67,8 @@ def tile_list_branch_max_combining_kernel(
         def cast(engine, out, in_):
             if engine == "scalar":
                 nc.scalar.activation(out, in_, COPY)
+            elif engine == "gpsimd":
+                nc.gpsimd.tensor_scalar(out, in_, 1.0, -0.0, op0=MULT, op1=ADD)
             else:
                 nc.vector.tensor_copy(out, in_)
 
@@ -215,8 +219,10 @@ def tile_list_branch_max_combining_kernel(
             for a in order:
                 times_v(a_acc, wa_q[a, t], wa_sc[a, t], a, s, a == order[0], a == order[1])
             nc.vector.tensor_tensor(h[:, t, HALF * s : HALF * (s + 1)], a_acc[:], b_sb[s, t], MAX)
-            if s == HALVES - 1:
-                nc.sync.dma_start(h_out[:, t, :], h[:, t, :])
+            if (s, t) == (HALVES - 1, 0):
+                nc.sync.dma_start(h_out[:, 0, :], h[:, 0, :])
+            elif t == PACK - 1:
+                nc.sync.dma_start(h_out[:, 1:PACK, HALF * s : HALF * (s + 1)], h[:, 1:PACK, HALF * s : HALF * (s + 1)])
 
         wy_q = {}
         wy_sc = sb([P, N], U8, "wy_sc")
@@ -255,15 +261,17 @@ def tile_list_branch_max_combining_kernel(
         quantize_wy(sb([P, P], U32, "wy_q0"), wy_bf0[:], 0, 1)
         eighths = [wy_raw[:, j, 0 : 2 * P].bitcast(BF16) for j in range(PACK)]
         for j in range(PACK):
-            round_h("scalar", eighths[j], P * j, P * (j + 1))
+            round_h("scalar" if j < PACK - 1 else "gpsimd", eighths[j], P * j, P * (j + 1))
         second = at(BF_AT, [P, HALF * PACK], BF16, "second")
         cut = HALF - SCALAR_TOKENS
         round_h("vector", second[:, 0 : PACK * cut], HALF, HALF + cut)
         round_h("scalar", second[:, PACK * cut :], HALF + cut, S)
         for j in range(PACK):
             quantize_h(eighths[j], P * j, P * (j + 1))
+        codes_out = out_2[0].rearrange("p m t -> p (m t)").bitcast(I32)
+        nc.sync.dma_start(codes_out[:, 0:HALF], h_q[:, 0:HALF].bitcast(I32))
         quantize_h(second[:], HALF, S)
-        nc.sync.dma_start(out_2[0].rearrange("p m t -> p (m t)").bitcast(I32), h_q[:].bitcast(I32))
+        nc.sync.dma_start(codes_out[:, HALF:S], h_q[:, HALF:S].bitcast(I32))
         quantize_wy(at(BF_AT + KB, [P, P], U32, "wy_q1"), wy_bf1[:], 1, 1)
         for first, offset in ((2, BF_AT - KB), (4, BF_AT + 3 * KB)):
             rounded = at(offset, [P, 2 * P * PACK], BF16, "wy_bf%d" % first)

@@ -28,7 +28,7 @@ HALVES = S // HALF
 N_TILES = N // P
 QUADS = 4
 BANKS = 8
-WARM_UPS = 6
+WARM_UPS = 5
 AHEAD = 11
 SC_ROWS = 32
 WD_ROW = 4
@@ -95,9 +95,11 @@ def tile_list_branch_max_combining_kernel(
         def load_scale_rows(tile, scales):
             nc.sync.dma_start(tile[0:SC_ROWS].bitcast(I32), scales.bitcast(I32).rearrange("a q c -> q a c"))
 
-        load_scale_rows(wb_sc_raw[:], wb_scales)
-        nc.sync.dma_start(offsets[:], offs)
         load_scale_rows(tab_sc[:], tab_scales)
+        nc.sync.dma_start(offsets[:], offs)
+        load_scale_rows(wb_sc_raw[:], wb_scales)
+        v_sc = at(V_SC_AT, [P, S], U8, "v_sc")
+        nc.vector.tensor_copy(v_sc[:], tab_sc[:].indirect(offsets[:]))
         wb_raw = sb([P, PASSES, H // 2], I32, "wb_raw")
         nc.sync.dma_start(wb_raw[:], wb_words.bitcast(I32).rearrange("a p c -> p a c"))
         tab = [load_tab(0)]
@@ -121,8 +123,6 @@ def tile_list_branch_max_combining_kernel(
         nc.tensor.transpose(by_cols[:], by_rows[:], identity[:])
         bias = sb([P, N_TILES], F32, "bias")
 
-        v_sc = at(V_SC_AT, [P, S], U8, "v_sc")
-        nc.vector.tensor_copy(v_sc[:], tab_sc[:].indirect(offsets[:]))
         nc.vector.tensor_copy(joined[:, 0:S].bitcast(I32), v_sc[:].bitcast(I32))
         for q in (0, 2, 1, 3):
             nc.sync.dma_start(both[32 * q : 32 * q + 4, :].bitcast(I32), joined[8 * q : 8 * q + 8, :].bitcast(I32))

@@ -29,7 +29,7 @@ N_TILES = N // P
 QUADS = 4
 BANKS = 8
 WARM_UPS = 5
-AHEAD = 11
+AHEAD = 10
 SC_ROWS = 32
 WD_ROW = 4
 H_ROW = 8
@@ -40,10 +40,12 @@ WA_AT = (12 * KB, 20 * KB)
 V_SC_AT = 19 * KB + 512
 TAB_AT = (28 * KB, 41 * KB)
 BF_AT = 50 * KB
-EARLY_GROUPS = 3
+EARLY_GROUPS = 2
 Y_BANKS = 8
 SCALAR_TOKENS = 176
 LEAD = 4
+WA_PARTS = (1, 2)
+LAST = 256
 
 
 def tile_list_branch_max_combining_kernel(
@@ -127,9 +129,15 @@ def tile_list_branch_max_combining_kernel(
         for q in (0, 2, 1, 3):
             nc.sync.dma_start(both[32 * q : 32 * q + 4, :].bitcast(I32), joined[8 * q : 8 * q + 8, :].bitcast(I32))
         wa_raw = []
-        for a in range(PASSES):
-            wa_raw.append(at(WA_AT[a], [P, PACK, H], F32, "wa_raw%d" % a))
-            nc.sync.dma_start(wa_raw[a][:], wa[512 * a : 512 * (a + 1), :].rearrange("(p j) c -> p j c", j=PACK))
+        for a, parts in enumerate(WA_PARTS):
+            rows = wa[512 * a : 512 * (a + 1), :].rearrange("(p j) c -> p j c", j=PACK)
+            width = H // parts
+            whole = at(WA_AT[a], [P, PACK * H], F32, "wa_raw%d" % a)
+            wa_raw.append([])
+            for part in range(parts):
+                piece = whole[:, PACK * width * part : PACK * width * (part + 1)].rearrange("p (j c) -> p j c", j=PACK)
+                nc.sync.dma_start(piece, rows[:, :, width * part : width * (part + 1)])
+                wa_raw[a].append(piece)
         nc.scalar.activation(bias[:], by_cols[:, 0:N_TILES], COPY)
 
         v = {}
@@ -162,13 +170,14 @@ def tile_list_branch_max_combining_kernel(
         for a in range(PASSES):
             nc.sync.dma_start(wd[:, a, :], wd_words[a].rearrange("p c i -> p (c i)").bitcast(I32))
 
-        def times_v(acc, lhsT, lhsT_scale, a, s, start, stop):
+        def times_v(acc, lhsT, lhsT_scale, a, lo, hi, start, stop):
+            s, first = divmod(lo, HALF)
             nc.tensor.matmul_mx(
-                out=acc[:],
+                out=acc[:, 0 : hi - lo],
                 lhsT=lhsT,
                 lhsT_scale=lhsT_scale,
-                rhs=v[a, s][:].bitcast(FP8X4),
-                rhs_scale=planes[a][:, HALF * s : HALF * (s + 1)],
+                rhs=v[a, s][:, first : first + hi - lo].bitcast(FP8X4),
+                rhs_scale=planes[a][:, lo:hi],
                 start=start,
                 stop=stop,
             )
@@ -181,19 +190,24 @@ def tile_list_branch_max_combining_kernel(
                     b_acc[s, t],
                     wb[a][:, 2 * P * t : 2 * P * (t + 1)].bitcast(FP4X4),
                     planes[a][:, S + P * t : S + P * (t + 1)],
-                    a, s, a == 0, a == PASSES - 1,
+                    a, HALF * s, HALF * (s + 1), a == 0, a == PASSES - 1,
                 )
 
         wa_q = {}
         wa_sc = {}
 
-        def quantize_wa(engine, a, t, slots):
-            rounded = sb([P, slots * P * PACK], BF16, "wa_bf%d_%d" % (a, t))
+        wa_bf = {(a, t): sb([P, 2 * P * PACK], BF16, "wa_bf%d_%d" % (a, t)) for a in range(PASSES) for t in (0, 2)}
+
+        def round_wa(engine, a, part, t):
+            count = P // WA_PARTS[a]
             cast(
                 engine,
-                rounded[:].rearrange("p (t m j) -> p m j t", t=slots, j=PACK),
-                wa_raw[a][:].rearrange("p j (m t) -> p m j t", t=PACK)[:, :, :, t : t + slots],
+                wa_bf[a, t][:].rearrange("p (t m j) -> p m j t", t=2, j=PACK)[:, count * part : count * (part + 1)],
+                wa_raw[a][part].rearrange("p j (m t) -> p m j t", t=PACK)[:, :, :, t : t + 2],
             )
+
+        def quantize_wa(a, t, slots):
+            rounded = wa_bf[a, t]
             codes = sb([P, slots * P], U32, "wa_q%d_%d" % (a, t))
             scales = sb([P, slots * P], U8, "wa_sc%d_%d" % (a, t))
             nc.vector.quantize_mx(out=codes[:].bitcast(FP8X4), scales=scales[:], in_=rounded[:])
@@ -201,10 +215,15 @@ def tile_list_branch_max_combining_kernel(
                 wa_q[a, t + u] = codes[:, P * u : P * (u + 1)].bitcast(FP8X4)
                 wa_sc[a, t + u] = scales[:, P * u : P * (u + 1)]
 
-        quantize_wa("scalar", 0, 0, 2)
-        quantize_wa("vector", 0, 2, 2)
-        quantize_wa("vector", 1, 0, 2)
-        quantize_wa("vector", 1, 2, 2)
+        round_wa("scalar", 0, 0, 0)
+        quantize_wa(0, 0, 2)
+        round_wa("vector", 0, 0, 2)
+        quantize_wa(0, 2, 2)
+        for part in range(WA_PARTS[1]):
+            for t in (0, 2):
+                round_wa("vector", 1, part, t)
+        for t in (0, 2):
+            quantize_wa(1, t, 2)
 
         b_tile = at(B_AT, [P, BANKS, HALF], F32, "b_sb")
         b_sb = {group: b_tile[:, index, :] for index, group in enumerate(groups)}
@@ -217,7 +236,7 @@ def tile_list_branch_max_combining_kernel(
             a_acc = bank(index, "a_acc%d" % index)
             order = (0, 1) if index < EARLY_GROUPS else (1, 0)
             for a in order:
-                times_v(a_acc, wa_q[a, t], wa_sc[a, t], a, s, a == order[0], a == order[1])
+                times_v(a_acc, wa_q[a, t], wa_sc[a, t], a, HALF * s, HALF * (s + 1), a == order[0], a == order[1])
             nc.vector.tensor_tensor(h[:, t, HALF * s : HALF * (s + 1)], a_acc[:], b_sb[s, t], MAX)
             if (s, t) == (HALVES - 1, 0):
                 nc.sync.dma_start(h_out[:, 0, :], h[:, 0, :])
@@ -280,23 +299,24 @@ def tile_list_branch_max_combining_kernel(
         for q in range(QUADS):
             nc.sync.dma_start(out_3[0, q : 16 : 4, :].bitcast(I32), h_sc[H_ROW + q : P : 32, :].bitcast(I32))
 
-        pieces = [(n, s) for n in range(N_TILES) for s in range(HALVES)]
+        pieces = [(n, HALF * s, HALF * (s + 1)) for n in range(N_TILES) for s in range(HALVES)][:-1]
+        pieces += [(N_TILES - 1, HALF, S - LAST), (N_TILES - 1, S - LAST, S)]
         res = [sb([P, S], F32, "y%d" % n) for n in range(N_TILES)]
         y_acc = {}
 
         def direct(index, a):
-            n, s = pieces[index]
+            n, lo, hi = pieces[index]
             if a == 0:
                 y_acc[index] = bank(index % Y_BANKS, "y_acc%d" % index)
             cols = slice(P * n, P * (n + 1))
-            times_v(y_acc[index], wd[:, a, cols].bitcast(FP8X4), wd_sc[WD_ROW:P, a, :].bitcast(U8)[:, cols], a, s, a == 0, False)
+            times_v(y_acc[index], wd[:, a, cols].bitcast(FP8X4), wd_sc[WD_ROW:P, a, :].bitcast(U8)[:, cols], a, lo, hi, a == 0, False)
 
         def close(index):
-            n, s = pieces[index]
+            n, lo, hi = pieces[index]
             cols = slice(P * n, P * (n + 1))
-            tokens = slice(HALF * s, HALF * (s + 1))
+            tokens = slice(lo, hi)
             nc.tensor.matmul_mx(
-                out=y_acc[index][:],
+                out=y_acc[index][:, 0 : hi - lo],
                 lhsT=wy_q[n],
                 lhsT_scale=wy_sc[:, cols],
                 rhs=h_q[:, tokens].bitcast(FP8X4),
@@ -304,10 +324,11 @@ def tile_list_branch_max_combining_kernel(
                 start=False,
                 stop=True,
             )
-            nc.scalar.activation(res[n][:, tokens], y_acc[index][:], TANH, bias=bias[:, n : n + 1])
-            if n == N_TILES - 1:
-                nc.sync.dma_start(out_0[cols, tokens], res[n][:, tokens])
-            elif s == HALVES - 1:
+            nc.scalar.activation(res[n][:, tokens], y_acc[index][:, 0 : hi - lo], TANH, bias=bias[:, n : n + 1])
+            if n == N_TILES - 1 and lo > 0:
+                first = 0 if hi < S else lo
+                nc.sync.dma_start(out_0[cols, first:hi], res[n][:, first:hi])
+            elif hi == S:
                 nc.sync.dma_start(out_0[cols, :], res[n][:])
 
         passes = [(index, a) for a in range(PASSES) for index in range(LEAD)]

@@ -325,9 +325,8 @@ def tile_list_branch_max_combining_kernel(
                 stop=True,
             )
             nc.scalar.activation(res[n][:, tokens], y_acc[index][:, 0 : hi - lo], TANH, bias=bias[:, n : n + 1])
-            if n == N_TILES - 1 and lo > 0:
-                first = 0 if hi < S else lo
-                nc.sync.dma_start(out_0[cols, first:hi], res[n][:, first:hi])
+            if n >= N_TILES - 2:
+                nc.sync.dma_start(out_0[cols, tokens], res[n][:, tokens])
             elif hi == S:
                 nc.sync.dma_start(out_0[cols, :], res[n][:])
 

from contextlib import ExitStack

import concourse.mybir as mybir
from concourse.masks import make_identity

T, S, K, H, N = 2048, 1024, 1024, 512, 768
FLOPS = 2 * S * (2 * K * H + H * N + K * N)

F32 = mybir.dt.float32
BF16 = mybir.dt.bfloat16
I32 = mybir.dt.int32
U32 = mybir.dt.uint32
U16 = mybir.dt.uint16
U8 = mybir.dt.uint8
FP8X4 = mybir.dt.float8_e4m3fn_x4
FP4X4 = mybir.dt.float4_e2m1fn_x4
COPY = mybir.ActivationFunctionType.Copy
TANH = mybir.ActivationFunctionType.Tanh
MAX = mybir.AluOpType.max
MULT = mybir.AluOpType.mult
ADD = mybir.AluOpType.add

P = 128
PACK = 4
PASSES = K // (P * PACK)
HALF = 512
HALVES = S // HALF
N_TILES = N // P
QUADS = 4
BANKS = 8
WARM_UPS = 5
AHEAD = 10
SC_ROWS = 32
WD_ROW = 4
H_ROW = 8
KB = 1024
ALIGN = 256
B_AT = 0
WA_AT = (12 * KB, 20 * KB)
V_SC_AT = 19 * KB + 512
TAB_AT = (28 * KB, 41 * KB)
BF_AT = 50 * KB
EARLY_GROUPS = 2
Y_BANKS = 8
SCALAR_TOKENS = 176
LEAD = 4
WA_PARTS = (1, 2)
LAST = 256


def tile_list_branch_max_combining_kernel(
    tc, tab_words, tab_scales, offs, wa, wb_words, wb_scales, wy, wd_words, wd_scales, by, out_0, out_1, out_2, out_3
):
    nc = tc.nc
    with ExitStack() as ctx:
        keep = ctx.enter_context(tc.tile_pool(name="keep", bufs=1))
        placed = ctx.enter_context(tc.tile_pool(name="placed", bufs=1))
        psum = ctx.enter_context(tc.psum_pool(name="psum", bufs=1))

        def sb(shape, dtype, name):
            return keep.tile(shape, dtype, name=name, align_bytes=ALIGN)

        def at(offset, shape, dtype, name):
            return placed.tile(shape, dtype, name=name, offset=offset, align_bytes=ALIGN)

        def bank(index, name):
            return psum.tile([P, HALF], F32, name=name, tag="bank%d" % index)

        def cast(engine, out, in_):
            if engine == "scalar":
                nc.scalar.activation(out, in_, COPY)
            elif engine == "gpsimd":
                nc.gpsimd.tensor_scalar(out, in_, 1.0, -0.0, op0=MULT, op1=ADD)
            else:
                nc.vector.tensor_copy(out, in_)

        offsets = keep.tile([P, S // 16], U16, name="offsets", align_bytes=ALIGN)
        tab_sc = sb([P, T], U8, "tab_sc")
        wb_sc_raw = sb([P, H], U8, "wb_sc_raw")
        for lo, hi in ((SC_ROWS, 64), (64, P)):
            nc.vector.memset(wb_sc_raw[lo:hi, :].bitcast(I32), 0)
            nc.vector.memset(tab_sc[lo:hi, :].bitcast(I32), 0)
        joined = sb([P, S + H], U8, "joined")
        both = sb([P, PASSES * (S + H)], U8, "planes")
        nc.vector.memset(both[:].bitcast(I32), 0)
        planes = [both[:, (S + H) * a : (S + H) * (a + 1)] for a in range(PASSES)]
        by_rows = sb([P, P], F32, "by_rows")
        nc.gpsimd.memset(by_rows[:], 0.0)
        identity = sb([P, P], F32, "identity")
        make_identity(nc, identity[:])

        def load_tab(a):
            tile = at(TAB_AT[a], [P, T], I32, "tab%d" % a)
            nc.sync.dma_start(tile[:], tab_words[a].rearrange("p t i -> p (t i)").bitcast(I32))
            return tile

        def load_scale_rows(tile, scales):
            nc.sync.dma_start(tile[0:SC_ROWS].bitcast(I32), scales.bitcast(I32).rearrange("a q c -> q a c"))

        load_scale_rows(tab_sc[:], tab_scales)
        nc.sync.dma_start(offsets[:], offs)
        load_scale_rows(wb_sc_raw[:], wb_scales)
        v_sc = at(V_SC_AT, [P, S], U8, "v_sc")
        nc.vector.tensor_copy(v_sc[:], tab_sc[:].indirect(offsets[:]))
        wb_raw = sb([P, PASSES, H // 2], I32, "wb_raw")
        nc.sync.dma_start(wb_raw[:], wb_words.bitcast(I32).rearrange("a p c -> p a c"))
        tab = [load_tab(0)]
        nc.sync.dma_start(by_rows[0:N_TILES, :], by.rearrange("(c p) -> c p", p=P))
        nc.vector.tensor_copy(
            joined[:, S : S + H].rearrange("p (t m) -> p t m", t=PACK),
            wb_sc_raw[:].rearrange("p (m t) -> p t m", t=PACK),
        )
        tab.append(load_tab(1))

        def deal_wb(dealt, a):
            nc.scalar.copy(
                dealt[:].bitcast(U16).rearrange("p (t m) -> p t m", t=PACK),
                wb_raw[:, a, :].bitcast(U16).rearrange("p (m t) -> p t m", t=PACK),
            )
            return dealt

        wb = [deal_wb(sb([P, 2 * H], U8, "wb0"), 0)]

        by_cols = psum.tile([P, P], F32, name="by_cols", tag="bank%d" % (BANKS - 1))
        nc.tensor.transpose(by_cols[:], by_rows[:], identity[:])
        bias = sb([P, N_TILES], F32, "bias")

        nc.vector.tensor_copy(joined[:, 0:S].bitcast(I32), v_sc[:].bitcast(I32))
        for q in (0, 2, 1, 3):
            nc.sync.dma_start(both[32 * q : 32 * q + 4, :].bitcast(I32), joined[8 * q : 8 * q + 8, :].bitcast(I32))
        wa_raw = []
        for a, parts in enumerate(WA_PARTS):
            rows = wa[512 * a : 512 * (a + 1), :].rearrange("(p j) c -> p j c", j=PACK)
            width = H // parts
            whole = at(WA_AT[a], [P, PACK * H], F32, "wa_raw%d" % a)
            wa_raw.append([])
            for part in range(parts):
                piece = whole[:, PACK * width * part : PACK * width * (part + 1)].rearrange("p (j c) -> p j c", j=PACK)
                nc.sync.dma_start(piece, rows[:, :, width * part : width * (part + 1)])
                wa_raw[a].append(piece)
        nc.scalar.activation(bias[:], by_cols[:, 0:N_TILES], COPY)

        v = {}
        for a in range(PASSES):
            for s in range(HALVES):
                v[a, s] = sb([P, HALF], U32, "v%d_%d" % (a, s))
                cols = HALF // 16
                nc.vector.tensor_copy(v[a, s][:], tab[a][:].bitcast(U32).indirect(offsets[:, cols * s : cols * (s + 1)]))

        warm = bank(BANKS - 2, "warm")
        for index in range(WARM_UPS):
            nc.tensor.matmul_mx(
                out=warm[:],
                lhsT=tab[0][:, 0:P].bitcast(FP8X4),
                lhsT_scale=tab_sc[:, 0:P],
                rhs=tab[0][:, 0:HALF].bitcast(FP8X4),
                rhs_scale=tab_sc[:, 0:HALF],
                start=True,
                stop=True,
            )

        wy_raw = at(TAB_AT[0] + 2 * H, [P, PACK, N], F32, "wy_raw")
        nc.sync.dma_start(wy_raw[:], wy.rearrange("(p j) n -> p j n", j=PACK))
        wb.append(deal_wb(at(TAB_AT[0], [P, 2 * H], U8, "wb1"), 1))
        wd_sc = wb_raw[:].rearrange("p a c -> p (a c)")[:, 0 : PASSES * N // 4].rearrange("p (a c) -> p a c", a=PASSES)
        wd_rows = wd_scales.bitcast(I32).rearrange("a (q r) c -> r q a c", r=4)
        for r in range(4):
            nc.sync.dma_start(wd_sc[WD_ROW + r : P : 32], wd_rows[r])
        wd = at(TAB_AT[1], [P, PASSES, N], I32, "wd")
        for a in range(PASSES):
            nc.sync.dma_start(wd[:, a, :], wd_words[a].rearrange("p c i -> p (c i)").bitcast(I32))

        def times_v(acc, lhsT, lhsT_scale, a, lo, hi, start, stop):
            s, first = divmod(lo, HALF)
            nc.tensor.matmul_mx(
                out=acc[:, 0 : hi - lo],
                lhsT=lhsT,
                lhsT_scale=lhsT_scale,
                rhs=v[a, s][:, first : first + hi - lo].bitcast(FP8X4),
                rhs_scale=planes[a][:, lo:hi],
                start=start,
                stop=stop,
            )

        groups = [(0, 0), (1, 0)] + [(s, t) for s in range(HALVES) for t in range(1, PACK)]
        b_acc = {group: bank(index, "b_acc%d" % index) for index, group in enumerate(groups)}
        for a in range(PASSES):
            for s, t in sorted(groups) if a == 0 else groups:
                times_v(
                    b_acc[s, t],
                    wb[a][:, 2 * P * t : 2 * P * (t + 1)].bitcast(FP4X4),
                    planes[a][:, S + P * t : S + P * (t + 1)],
                    a, HALF * s, HALF * (s + 1), a == 0, a == PASSES - 1,
                )

        wa_q = {}
        wa_sc = {}

        wa_bf = {(a, t): sb([P, 2 * P * PACK], BF16, "wa_bf%d_%d" % (a, t)) for a in range(PASSES) for t in (0, 2)}

        def round_wa(engine, a, part, t):
            count = P // WA_PARTS[a]
            cast(
                engine,
                wa_bf[a, t][:].rearrange("p (t m j) -> p m j t", t=2, j=PACK)[:, count * part : count * (part + 1)],
                wa_raw[a][part].rearrange("p j (m t) -> p m j t", t=PACK)[:, :, :, t : t + 2],
            )

        def quantize_wa(a, t, slots):
            rounded = wa_bf[a, t]
            codes = sb([P, slots * P], U32, "wa_q%d_%d" % (a, t))
            scales = sb([P, slots * P], U8, "wa_sc%d_%d" % (a, t))
            nc.vector.quantize_mx(out=codes[:].bitcast(FP8X4), scales=scales[:], in_=rounded[:])
            for u in range(slots):
                wa_q[a, t + u] = codes[:, P * u : P * (u + 1)].bitcast(FP8X4)
                wa_sc[a, t + u] = scales[:, P * u : P * (u + 1)]

        round_wa("scalar", 0, 0, 0)
        quantize_wa(0, 0, 2)
        round_wa("vector", 0, 0, 2)
        quantize_wa(0, 2, 2)
        for part in range(WA_PARTS[1]):
            for t in (0, 2):
                round_wa("vector", 1, part, t)
        for t in (0, 2):
            quantize_wa(1, t, 2)

        b_tile = at(B_AT, [P, BANKS, HALF], F32, "b_sb")
        b_sb = {group: b_tile[:, index, :] for index, group in enumerate(groups)}
        for group in groups:
            nc.scalar.activation(b_sb[group], b_acc[group][:], COPY)

        h = sb([P, PACK, S], F32, "h")
        h_out = out_1.rearrange("(p t) j -> p t j", t=PACK)
        for index, (s, t) in enumerate(groups):
            a_acc = bank(index, "a_acc%d" % index)
            order = (0, 1) if index < EARLY_GROUPS else (1, 0)
            for a in order:
                times_v(a_acc, wa_q[a, t], wa_sc[a, t], a, HALF * s, HALF * (s + 1), a == order[0], a == order[1])
            nc.vector.tensor_tensor(h[:, t, HALF * s : HALF * (s + 1)], a_acc[:], b_sb[s, t], MAX)
            if (s, t) == (HALVES - 1, 0):
                nc.sync.dma_start(h_out[:, 0, :], h[:, 0, :])
            elif t == PACK - 1:
                nc.sync.dma_start(h_out[:, 1:PACK, HALF * s : HALF * (s + 1)], h[:, 1:PACK, HALF * s : HALF * (s + 1)])

        wy_q = {}
        wy_sc = sb([P, N], U8, "wy_sc")

        def round_wy(engine, rounded, first, tiles):
            cast(
                engine,
                rounded.rearrange("p (c i j) -> p c j i", i=4, j=PACK),
                wy_raw[:, :, P * first : P * (first + tiles)].rearrange("p j (c i) -> p c j i", i=4),
            )

        def quantize_wy(codes, rounded, first, tiles):
            nc.vector.quantize_mx(out=codes[:].bitcast(FP8X4), scales=wy_sc[:, P * first : P * (first + tiles)], in_=rounded)
            for n in range(tiles):
                wy_q[first + n] = codes[:, P * n : P * (n + 1)].bitcast(FP8X4)

        def round_h(engine, rounded, lo, hi):
            if hi <= HALF:
                cast(engine, rounded.rearrange("p (c t) -> p c t", t=PACK), h[:, :, lo:hi].rearrange("p t c -> p c t"))
            else:
                cast(
                    engine,
                    rounded.rearrange("p (c i t) -> p c t i", i=4, t=PACK),
                    h[:, :, lo:hi].rearrange("p t (c i) -> p c t i", i=4),
                )

        def quantize_h(rounded, lo, hi):
            nc.vector.quantize_mx(out=h_q[:, lo:hi].bitcast(FP8X4), scales=h_sc[H_ROW:P, lo:hi], in_=rounded)

        h_q = sb([P, S], U32, "h_q")
        h_sc = sb([P, S], U8, "h_sc")
        wy_bf0 = at(BF_AT, [P, P * PACK], BF16, "wy_bf0")
        wy_bf1 = sb([P, P * PACK], BF16, "wy_bf1")
        round_wy("scalar", wy_bf0[:], 0, 1)
        round_wy("scalar", wy_bf1[:], 1, 1)
        quantize_wy(sb([P, P], U32, "wy_q0"), wy_bf0[:], 0, 1)
        eighths = [wy_raw[:, j, 0 : 2 * P].bitcast(BF16) for j in range(PACK)]
        for j in range(PACK):
            round_h("scalar" if j < PACK - 1 else "gpsimd", eighths[j], P * j, P * (j + 1))
        second = at(BF_AT, [P, HALF * PACK], BF16, "second")
        cut = HALF - SCALAR_TOKENS
        round_h("vector", second[:, 0 : PACK * cut], HALF, HALF + cut)
        round_h("scalar", second[:, PACK * cut :], HALF + cut, S)
        for j in range(PACK):
            quantize_h(eighths[j], P * j, P * (j + 1))
        codes_out = out_2[0].rearrange("p m t -> p (m t)").bitcast(I32)
        nc.sync.dma_start(codes_out[:, 0:HALF], h_q[:, 0:HALF].bitcast(I32))
        quantize_h(second[:], HALF, S)
        nc.sync.dma_start(codes_out[:, HALF:S], h_q[:, HALF:S].bitcast(I32))
        quantize_wy(at(BF_AT + KB, [P, P], U32, "wy_q1"), wy_bf1[:], 1, 1)
        for first, offset in ((2, BF_AT - KB), (4, BF_AT + 3 * KB)):
            rounded = at(offset, [P, 2 * P * PACK], BF16, "wy_bf%d" % first)
            round_wy("vector", rounded[:], first, 2)
            quantize_wy(sb([P, 2 * P], U32, "wy_q%d" % first), rounded[:], first, 2)
        for q in range(QUADS):
            nc.sync.dma_start(out_3[0, q : 16 : 4, :].bitcast(I32), h_sc[H_ROW + q : P : 32, :].bitcast(I32))

        pieces = [(n, HALF * s, HALF * (s + 1)) for n in range(N_TILES) for s in range(HALVES)][:-1]
        pieces += [(N_TILES - 1, HALF, S - LAST), (N_TILES - 1, S - LAST, S)]
        res = [sb([P, S], F32, "y%d" % n) for n in range(N_TILES)]
        y_acc = {}

        def direct(index, a):
            n, lo, hi = pieces[index]
            if a == 0:
                y_acc[index] = bank(index % Y_BANKS, "y_acc%d" % index)
            cols = slice(P * n, P * (n + 1))
            times_v(y_acc[index], wd[:, a, cols].bitcast(FP8X4), wd_sc[WD_ROW:P, a, :].bitcast(U8)[:, cols], a, lo, hi, a == 0, False)

        def close(index):
            n, lo, hi = pieces[index]
            cols = slice(P * n, P * (n + 1))
            tokens = slice(lo, hi)
            nc.tensor.matmul_mx(
                out=y_acc[index][:, 0 : hi - lo],
                lhsT=wy_q[n],
                lhsT_scale=wy_sc[:, cols],
                rhs=h_q[:, tokens].bitcast(FP8X4),
                rhs_scale=h_sc[H_ROW:P, tokens],
                start=False,
                stop=True,
            )
            nc.scalar.activation(res[n][:, tokens], y_acc[index][:, 0 : hi - lo], TANH, bias=bias[:, n : n + 1])
            if n >= N_TILES - 2:
                nc.sync.dma_start(out_0[cols, tokens], res[n][:, tokens])
            elif hi == S:
                nc.sync.dma_start(out_0[cols, :], res[n][:])

        passes = [(index, a) for a in range(PASSES) for index in range(LEAD)]
        passes += [(index, a) for index in range(LEAD, len(pieces)) for a in range(PASSES)]
        done = 0
        for index in range(len(pieces)):
            upto = max(AHEAD + index, PASSES * (index + 1))
            for later, a in passes[done:upto]:
                direct(later, a)
            done = upto
            close(index)
